import numpy as np, ml_dtypes
CORES = [16,17,18,19,32,33,34,35]
N = 8
import mx_ref
BF = ml_dtypes.bfloat16
def pick(q, e):
    c = np.concatenate([q[0].reshape(128, -1, 4), np.zeros((128, 1, 4), np.uint8)], axis=1); s = np.concatenate([q[1], np.ones((16, 1), np.uint8)], axis=1)
    return (np.ascontiguousarray(c[:, e].reshape(128, -1)), np.ascontiguousarray(s[:, e]))
def join(*qs):
    return (np.concatenate([q[0] for q in qs], axis=1), np.concatenate([q[1] for q in qs], axis=1))
def put(q, e, v):
    c, s = q[0].reshape(128, -1, 4).copy(), q[1].copy(); c[:, e] = v[0].reshape(128, -1, 4); s[:, e] = v[1]
    return (c.reshape(128, -1), s)
def pk(c, s):
    return (np.ascontiguousarray(c), mx_ref.live(s))
def emit(q):
    return q[0], q[1]
def tile(rs):
    return np.stack(rs, axis=2).reshape(128, -1).astype(BF)
def cut(t, i, w=512):
    return t[:, w * i:w * i + w]
def f(rng, *shape):
    return mx_ref.flush((rng.standard_normal(shape, dtype=np.float32) * np.exp2(rng.integers(-2, 3, shape[:-1] + (1,)))).astype(BF))
def wide(rng, *shape, cols=0):
    v = rng.standard_normal(shape, dtype=np.float32) * np.exp2(rng.integers(-12, 13, shape)).astype(np.float32)
    if cols: v *= np.repeat(np.exp2(rng.integers(-cols, cols + 1, shape[:-2] + (1, shape[-1] // 4))) * (rng.random(shape[:-2] + (1, shape[-1] // 4)) > 0.0625), 4, axis=-1).astype(np.float32)
    return mx_ref.flush(v.astype(BF))
P, CAPP, L, CB = 256, 64, 3, 64
def big(v, k):
    v = v.astype(np.float32) * np.float32(k)
    v[np.abs(v) < np.float32(2.0 ** -10)] = 0
    return v.astype(BF)
def number(z):
    n = np.zeros(z.shape[1], np.int64)
    for b in range(L): n += (z[b] < 0) * (1 << b)
    return n
def buckets(x, pl):
    X = [mx_ref.quantize(np.ascontiguousarray(x[s])) for s in range(N)]
    return X, np.stack([number(mx_ref.matmul(mx_ref.quantize(np.ascontiguousarray(pl[s])), X[s])) for s in range(N)])
def taken(bk):
    at = np.full((N, N, CAPP), -1)
    for d in range(N):
        for s in range(N):
            e = np.flatnonzero(bk[s] == d)[:CAPP]
            at[d, s, :e.size] = e
    return at
def attend(c, wv, e):
    e = np.concatenate([e, np.setdiff1d(np.arange(512), e)[:max(4 - len(e), len(e) % 2)]])
    m = pick(c, e)
    ct = [pick(c, np.arange(t, 512, 4)) for t in range(4)]
    A = tile([np.float32(0.0625) * np.maximum(mx_ref.matmul(k, m) + np.float32(0), np.float32(0)) for k in ct])
    qw = mx_ref.quantize(np.ascontiguousarray(wv))
    V = tile([mx_ref.matmul(k, qw) for k in ct])
    qa = mx_ref.quantize(A)
    O = [mx_ref.matmul(mx_ref.quantize(np.ascontiguousarray(cut(V, i))), qa) for i in range(4)]
    h = np.zeros((128, 512, 4), BF)
    h[:, e] = tile([np.float32(0.0625) * o for o in O]).reshape(128, -1, 4)
    return A, V, h.reshape(128, 2048)
def planes(rng):
    p = np.array(f(rng, 128, 512))
    p[:, 4 * L:] = 0
    return np.stack([p] * N)
def plain(rng):
    return {"x": big(f(rng, N, 128, 4 * P), 0.25), "pl": planes(rng), "p2": planes(rng), "wv": big(f(rng, N, 128, 2048), 0.25), "w": f(rng, N, 128, 512)}
def aimed(rng, d, want, gone=0, then=None, two=None):
    x, p = d["x"].astype(np.float32).reshape(N, 128, P, 4), np.zeros((128, 128, 4), np.float32)
    gone = np.zeros((N, P), np.int64) + gone
    at = rng.permutation(128)[:16 * L + 16].reshape(L + 1, 16)
    side = np.zeros((N, 128, 4), np.float32)
    for b in range(L):
        v = (1 + rng.random((16, 4))) * rng.choice([-1.0, 1.0], (16, 4))
        p[at[b], b] = v
        turn = (1 - 2 * (want >> b & 1)) * (1 - (gone >> b & 1))
        x[:, at[b]] = np.abs(x[:, at[b]]) * (np.sign(v)[None, :, None, :] * turn[:, None, :, None]) * (0.0625 if then is None else 1.0)
        side[:, at[b]] = np.sign(v)[None] * (1 - 2 * (np.arange(N) >> b & 1))[:, None, None]
    parted = np.zeros((128, 4), np.float32)
    if two is not None:
        k = two[2][:, None, :, None]
        u = rng.choice([-1.0, 1.0], (16, 4))
        parted[at[L]] = u
        x = np.where(k != 0, np.float32(0.125) * x, x)
        x[:, at[L]] = np.where(k != 0, 0.5 * (1 + rng.random((N, 16, P, 4))) * u[None, :, None, :] * k, x[:, at[L]])
    x = x * (gone != N - 1)[:, None, :, None]
    d = {**d, "x": big(x.reshape(N, 128, 4 * P), 1), "pl": np.stack([p.reshape(128, 512).astype(BF)] * N)}
    if then is None: return d
    p2, wv = np.zeros((128, 128, 4), np.float32), d["wv"].astype(np.float32).reshape(N, 128, 4, 128, 4)
    on = rng.permutation(128)[:16 * L].reshape(L, 16)
    for b in range(L):
        p2[on[b], b] = 1 + rng.random((16, 4))
        for q in range(N):
            sign = parted if two is not None and q == two[0] and b == two[1] else side[q]
            wv[q][:, :, on[b]] = np.abs(wv[q][:, :, on[b]]) * sign[:, None, None, :] * (1 - 2 * (int(then[q]) >> b & 1))
    return {**d, "wv": big(wv.reshape(N, 128, 2048), 1), "p2": np.stack([p2.reshape(128, 512).astype(BF)] * N)}
def setup_inputs(rng):
    return plain(rng)
def setup_inputs_crowd(rng):
    h, g = (int(v) for v in rng.permutation(N)[:2])
    c, then = rng.permutation(N), np.zeros(N, np.int64)
    then[c] = np.roll(c, 1)
    bit = int(rng.choice([b for b in range(L) if int(then[h]) ^ (1 << b) != h]))
    one = int(rng.choice([q for q in range(N) if q not in (h, g) and int(then[q]) != int(then[h]) ^ (1 << bit)]))
    others = np.delete(np.arange(N), [h, g, one])
    o, n = rng.permutation(N), np.full(N, CAPP)
    n[o[N // 2:]] += rng.integers(1, P - CAPP + 1, N - N // 2)
    n[o[-1]] = P
    r, more = int(o[N // 2]), P // (CAPP + 1) - 1
    if more: n[r] = rng.integers(CAPP + 1, P - more * (CAPP + 1) + 1)
    want = rng.choice(others, (N, P))
    for s in range(N): want[s, rng.permutation(P)[:n[s]]] = h
    e = rng.permutation(np.flatnonzero((want != h) & (np.arange(N) != r)[:, None]))
    want.flat[e[:CB]] = g
    want.flat[e[CB]] = one
    if more:
        e = rng.permutation(np.flatnonzero(want[r] != h))
        want[r, e[:more * (CAPP + 1)]] = np.repeat(rng.choice(others, more, replace=False), CAPP + 1)
    kind = np.zeros((N, P), np.int64)
    for s in range(N):
        e = np.flatnonzero(want[s] == h)
        kind[s, e] = 1 - 2 * ((np.arange(e.size) + int(rng.integers(0, 2))) % 2)
    return aimed(rng, plain(rng), want, then=then, two=(h, bit, kind))
def setup_inputs_few(rng):
    o = rng.permutation(N)
    want = rng.choice(o[2:], (N, P))
    want[int(rng.integers(0, N)), int(rng.integers(0, P))] = o[0]
    return aimed(rng, plain(rng), want)
def setup_inputs_neg(rng):
    d, g = plain(rng), rng.permutation(16)
    want = np.stack([rng.permutation(P) % N for s in range(N)])
    part = 8 * g[:, None] + np.arange(8)
    rows = (4 * part[L:].reshape(-1)[:, None] + np.arange(4)).reshape(-1)
    x, p = np.zeros((N, P, 512)), np.zeros((128, 128, 4))
    for b in range(L):
        v = rng.choice([-1.0, 1.0], (8, 4))
        p[part[b], b] = v * (1 + rng.random((8, 4)))
        e = (4 * part[b][:, None] + np.arange(4)).reshape(-1)
        x[:, :, e] = 2.0 ** -8 * v.reshape(-1) * (1 - 2 * (want >> b & 1))[:, :, None]
    for q in range(N):
        s, i = np.nonzero(want == q)
        v = np.full((P, P), -2.0 ** -7)
        v[np.arange(P), np.arange(P)] = P * 2.0 ** -7
        x[s[:, None], i[:, None], rng.permutation(rows)[:P][None, :]] = v * rng.choice([-1.0, 1.0], P)
    x *= np.exp2(rng.integers(-1, 2, (N, P, 1)))
    x = np.ascontiguousarray(x.reshape(N, P, 128, 4).transpose(0, 2, 1, 3)).reshape(N, 128, 4 * P)
    return {**d, "x": x.astype(np.float32).astype(BF), "pl": np.stack([p.reshape(128, 512).astype(np.float32).astype(BF)] * N)}
def setup_inputs_zero(rng):
    gone = np.zeros((N, P), np.int64)
    for s in range(N):
        e = rng.permutation(P)
        gone[s, e[:P // 4]] = N - 1
        gone[s, e[P // 4:P // 2]] = 1 << rng.integers(0, L, P // 2 - P // 4)
    d = aimed(rng, plain(rng), rng.integers(0, N, (N, P)), gone)
    b, q, on = int(rng.integers(0, L)), int(rng.integers(0, N)), rng.permutation(128)[:16]
    p2, wv = np.array(d["p2"]).reshape(N, 128, 128, 4), np.array(d["wv"]).reshape(N, 128, 4, 128, 4)
    p2[:, np.setdiff1d(np.arange(128), on), b] = 0
    wv[q][:, :, on] = 0
    return {**d, "p2": p2.reshape(N, 128, 512), "wv": wv.reshape(N, 128, 2048)}
def setup_inputs_spread(rng):
    return {**plain(rng), "x": big(wide(rng, N, 128, 4 * P, cols=2), 2.0 ** -10)}
def check_inputs(d):
    b = []
    for k in ("x", "pl", "p2", "wv", "w"):
        v = np.abs(d[k].astype(np.float32))
        if not (np.isfinite(v).all() and ((v == 0) | (v >= 2.0 ** -30) & (v <= 2.0 ** 30)).all()): b.append("a value of " + k)
    for k in ("pl", "p2"):
        p = d[k].astype(np.float32)
        if (p[:, :, 4 * L:] != 0).any(): b.append(k + " has numbers behind its first L columns")
        if (p != p[:1]).any(): b.append(k + " isn't the same on all ranks")
    return b
def reference(x, pl, p2, wv, w):
    X, bk = buckets(x, pl)
    at = taken(bk)
    H, num, to = [], [], []
    for d in range(N):
        c = join(*[pick(X[s], at[d, s]) for s in range(N)])
        A, V, h = attend(c, wv[d], np.flatnonzero(at[d].reshape(-1) >= 0))
        h = mx_ref.quantize(h)
        n = np.concatenate([np.where(at[d, s] >= 0, P * s + at[d, s], -1) for s in range(N)])
        H.append(h)
        num.append(n)
        to.append(np.where(n >= 0, number(mx_ref.matmul(mx_ref.quantize(np.ascontiguousarray(p2[d])), h)), -1))
    H = join(*H)
    num = np.concatenate(num + [np.full(1, -1)])
    oc, osc = np.zeros((N, 128, 4 * N * CB), np.uint8), np.zeros((N, 16, N * CB), np.uint8)
    nb, y = np.zeros((N, 1, N * CB), np.float32), np.zeros((N, 128, N * CB), np.float32)
    for e in range(N):
        k = np.full(N * CB, -1)
        for d in range(N):
            i = np.flatnonzero(to[d] == e)[:CB]
            k[d * CB + np.arange(i.size)] = 512 * d + i
        h = pick(H, k)
        oc[e], osc[e] = emit(h)
        nb[e, 0] = num[k]
        y[e] = mx_ref.matmul(mx_ref.quantize(np.ascontiguousarray(w[e])), h)
    return {"oc": oc, "osc": osc, "id": nb, "y": y}

@@ -1,0 +1,381 @@
+from concourse.bass import DstId, RemoteDMATransfer
+from concourse.mybir import dt, AluOpType, AxisListType, ActivationFunctionType
+
+NV = 8
+RV = (1, 2)
+HV = (2, 2)
+WL, WB = 64, 512
+
+BF, F4, I4, U2, CO, PL = "bfloat16", "float32", "int32", "uint16", "float8_e4m3fn_x4", "uint8"
+SCRATCH = {}
+for _n, _w, _d in (("zr", 256, BF), ("rp", 2048, BF), ("xt", 1032, BF), ("plt", 512, BF), ("p2t", 512, BF),
+                   ("wvt", 2048, BF), ("wt", 512, BF), ("vt", 2048, BF), ("at", 2048, BF), ("ht", 2056, BF),
+                   ("yt", 512, F4), ("ii", 16, I4), ("fpl", 24, F4), ("offpl", 24, U2), ("i16", 16, F4), ("cf", 16, F4),
+                   ("thr", 16, BF), ("thb", 16, F4), ("dcol", 2, BF), ("dcol2", 2, BF), ("ict", 32, F4), ("fct", 32, F4), ("offct", 32, U2),
+                   ("ip2", 16, F4), ("fp2", 32, F4), ("offp2", 32, U2), ("iu", 32, I4), ("iua", 32, I4), ("iuq", 32, F4), ("iue", 32, F4),
+                   ("iug", 32, F4), ("um", 32, BF), ("itr", 16, F4), ("tri", 16, F4), ("idj", 256, F4), ("dj", 256, F4), ("rp8", 128, BF),
+                   ("fg", 4, F4), ("offg", 2, U2), ("ll1", 32, F4), ("lt1", 32, F4), ("off1", 32, U2), ("off2", 32, U2), ("le", 16, F4),
+                   ("lf", 16, F4), ("lid", 16, F4), ("iv", 128, F4), ("eb", 128, BF), ("et", 128, BF), ("te", 16, F4), ("idw", 520, F4),
+                   ("u1", 768, BF), ("k1", 1024, BF), ("z1", 2048, BF), ("zs1", 2048, BF), ("jk1", 4096, BF), ("acc1", 16, F4), ("cn1", 16, F4),
+                   ("u2", 384, BF), ("k2", 512, BF), ("bc", 32, BF), ("bt", 32, BF), ("og", 2, F4), ("pp", 128, F4), ("pm", 128, F4),
+                   ("pt", 128, F4), ("pc", 128, F4), ("pf", 16, F4), ("pos", 16, U2), ("wn", 8 * WB + 256, F4), ("wtr", 512, F4),
+                   ("lz", 32, F4), ("lzt", 32, F4), ("lx", 64, F4), ("lxt", 64, F4), ("g16", 16, F4), ("off3", 16, U2), ("idsel", 64, F4)):
+    SCRATCH[_n] = ("sbuf", [128, _w], _d)
+for _n, _m, _w in (("xq", "xs", 258), ("plr", "plrs", 128), ("plq", "pls", 384), ("p2r", "p2rs", 128), ("p2q", "p2s", 480), ("wvq", "wvs", 512),
+                   ("wq", "ws", 128), ("send1", "send1s", 512), ("land1", "land1s", 512), ("ctq", "cts", 512), ("vq", "vs", 512),
+                   ("aq", "asc", 512), ("hq", "hs", 514), ("send2", "send2s", 512), ("land2", "land2s", 512)):
+    SCRATCH[_n] = ("sbuf", [128, _w], CO)
+    SCRATCH[_m] = ("sbuf", [128, _w], PL)
+for _n, _w in (("lst1", 4), ("ldl1", 8), ("lst2", 4), ("ldl2", 8)):
+    SCRATCH[_n] = ("dram", [_w, 128, 1], F4)
+for _h in range(8):
+    SCRATCH["ps%d" % _h] = ("psum", [128, 512], F4)
+SEMAPHORES = ["v", "s", "t", "gi", "dx", "dpl", "dwv", "dw", "dp2", "dl1", "do1", "div", "did0", "dl2", "do2", "did",
+              "doc", "dos", "dy", "snd", "a1", "l1", "a2on", "a2off", "l2"]
+
+
+def rank_program(g, core, T, topo):
+    r = T.rank_of(core)
+    if r is None:
+        return
+    cores = T.cores
+    n_ranks = len(cores)
+    Q = {"v": g.vector, "s": g.scalar, "t": g.tensor, "y": g.sync, "g": g}
+    V, S, PE = g.vector, g.scalar, g.tensor
+    op, fn = AluOpType, ActivationFunctionType
+    waited, count = {}, {}
+
+    def need(q, deps):
+        best = {}
+        for d in deps:
+            if d is not None:
+                best[d[0]] = max(best.get(d[0], 0), d[1])
+        for s in best:
+            if waited.get((q, s), 0) < best[s]:
+                Q[q].wait_ge(T.sem[s], best[s])
+                waited[(q, s)] = best[s]
+
+    def raised(ins, s, n):
+        ins.then_inc(T.sem[s], n)
+        count[s] = count.get(s, 0) + n
+        return (s, count[s])
+
+    def v(deps, f, *a):
+        need("v", deps)
+        return raised(f(*a), "v", 1)
+
+    def s(deps, out, in_, func, **k):
+        need("s", deps)
+        return raised(S.activation(out, in_, func, **k), "s", 1)
+
+    def mm(deps, out, a, asc, b, bsc, start=True, stop=True):
+        need("t", deps)
+        return raised(PE.matmul_mx(out, a, asc, b, bsc, start, stop), "t", 1)
+
+    def dma(q, deps, sem, out, in_):
+        need(q, deps)
+        return raised(Q[q].dma_start(out, in_), sem, 16)
+
+    def io(pat, out, base=0, ch=0, fl=True):
+        if fl:
+            return raised(g.iota(out, pat, base, ch, allow_small_or_imprecise_dtypes=True), "gi", 1)
+        return raised(g.iota(out, pat, base, ch), "gi", 1)
+
+    def ts(deps, out, in0, s1, s2, *ops):
+        return v(deps, V.tensor_scalar, out, in0, s1, s2, *ops)
+
+    def tt(deps, out, a, b, o):
+        return v(deps, V.tensor_tensor, out, a, b, o)
+
+    def cp(deps, out, in_):
+        return v(deps, V.tensor_copy, out, in_)
+
+    def fill(out, c):
+        return v([], V.memset, out, c)
+
+    def turn(deps, out, in_):
+        return v(deps, V.transpose, out, in_)
+
+    def scan(deps, *a):
+        return v(deps, V.tensor_tensor_scan, *a)
+
+    near = [q for q in range(n_ranks) if topo.chip(cores[q]) == topo.chip(core)]
+    far = [q for q in range(n_ranks) if q not in near]
+    near_to = [q for q in near if q != r]
+    n0, f0 = min(near), min(far)
+    far_pool = topo.engines(core, cores[far[0]])
+    near_pool = [e for e in topo.engines(core, cores[near_to[0]]) if e not in far_pool]
+
+    def share(pool, k):
+        w = 1
+        while 2 * w * k <= len(pool):
+            w *= 2
+        return w
+
+    wf, wn = share(far_pool, len(far)), share(near_pool, len(near_to))
+    eng = {}
+    for i, q in enumerate(far):
+        eng[q] = far_pool[wf * i:wf * i + wf]
+    for i, q in enumerate(near_to):
+        eng[q] = near_pool[wn * i:wn * i + wn]
+
+    def send(to, src_of, dst_of, sem_of, few=False):
+        tr = []
+        for q in to:
+            mask = 0
+            for e in eng[q][0:1] if few else eng[q]:
+                mask += 1 << e
+                count["snd"] = count.get("snd", 0) + 1
+            rid, pid, _ = topo.addr(cores[q])
+            tr.append(RemoteDMATransfer(dst_ids=[DstId(rid=rid, pnc=pid)], dma_engine_mask=mask, remote_sem=T.sem[sem_of(q)], src=src_of(q), dst=dst_of(q)))
+        g.remote_dma_fused(tr, local_sem=T.sem.snd)
+
+    dpl = dma("s", [], "dpl", T.plt[:, 0:16], T.pl[:, 0:16])
+    dx = dma("y", [], "dx", T.xt[:, 0:1024], T.x[:])
+    dwv = dma("y", [dx], "dwv", T.wvt[:], T.wv[:])
+    dw = dma("y", [], "dw", T.wt[:], T.w[:])
+    dp2 = dma("y", [], "dp2", T.p2t[:, 0:16], T.p2[:, 0:16])
+
+    i0 = io([[1, 1]], T.ii[:, 0:1], 0, 1, False)
+    ip = io([[1, 3], [0, 8]], T.fpl[:])
+    i1 = io([[1, 16]], T.i16[:])
+    ir = io([[0, 2048]], T.rp[:], base=1)
+    i2 = io([[1, 4], [64, 8]], T.ict[:])
+    i3 = io([[-1, 3], [0, 5]], T.ip2[:, 0:15], base=3)
+    i4 = io([[1, 32]], T.iu[:], 128, -1, False)
+    i5 = io([[1, 4], [0, 8]], T.iuq[:])
+    i6 = io([[16, 16]], T.itr[:], base=8 * WB)
+    i7 = io([[32, 4], [128, 4], [1, 16]], T.idj[:], base=-512)
+    pz = fill(T.plt[:, 16:512], 0.0)
+    xz = fill(T.xt[:, 1024:1032], 0.0)
+    p = T.ii[:, 0:1]
+    c1 = ts([i0], T.ii[:, 1:2], p, 31, 2, op.bitwise_and, op.arith_shift_right)
+    c2 = ts([], T.ii[:, 2:3], p, 3, None, op.bitwise_and)
+    opl = cp([ip], T.offpl[:], T.fpl[:])
+    dcol = ts([c1], T.dcol[:, 0:1], T.ii[:, 1:2], 8.0, None, op.subtract)
+    f1 = ts([c2], T.cf[:, 1:2], T.ii[:, 2:3], 16.0, None, op.mult)
+    zr = fill(T.zr[:], 0.0)
+    thr = ts([i1, f1], T.thr[:], T.i16[:], T.cf[:, 1:2], None, op.add)
+    thb = ts([i1, f1], T.thb[:], T.i16[:], T.cf[:, 1:2], 0.5, op.add, op.add)
+
+    def pick(deps, dq, ds, c0, wq_, ws_, wn_, off, e0, n):
+        e1 = e0 + n // 16
+        a = cp(deps, dq[:, c0:c0 + n].bitcast(dt.uint32), wq_[:, 0:wn_].bitcast(dt.uint32).indirect(off[:, e0:e1]))
+        b = s(deps, ds[:, c0:c0 + n], ws_[:, 0:wn_].indirect(off[:, e0:e1]), fn.Copy)
+        return [a, b]
+
+    plr = v([dpl, pz], V.quantize_mx, T.plr[:], T.plrs[:], T.plt[:])
+    plq = pick([plr, opl], T.plq, T.pls, 0, T.plr, T.plrs, 128, T.offpl, 0, 384)
+    xq = v([dx, xz], V.quantize_mx, T.xq[:], T.xs[:], T.xt[:])
+
+    zt = [mm(plq + [xq], T["ps%d" % b][:, 0:256], T.plq[:, 128 * b:128 * b + 128], T.pls[:, 128 * b:128 * b + 128], T.xq[:, 0:256], T.xs[:, 0:256]) for b in range(3)]
+
+    def number(zt, zp, u, k, w, dc, deps):
+        a, b, c = [ts([zt[i]], u[:, w * i:w * i + w], zp[i][:, 0:w], 0.0, lo, op.is_lt, m)
+                   for i, (lo, m) in enumerate(((-8.0, op.add), (2.0, op.mult), (4.0, op.mult)))]
+        d = scan([a, b], k[:, 0:w], u[:, w:2 * w], u[:, 0:w], -100.0, op.max, op.add)
+        e = scan([c, d], k[:, w:2 * w], u[:, 2 * w:3 * w], k[:, 0:w], -100.0, op.max, op.add)
+        return ts([e] + deps, k[:, 2 * w:3 * w], k[:, w:2 * w], dc, None, op.is_equal)
+
+    f = number(zt, [T.ps0, T.ps1, T.ps2], T.u1, T.k1, 256, T.dcol[:, 0:1], [dcol])
+    ct = scan([f, zr], T.k1[:, 768:1024], T.k1[:, 512:768], T.zr[:, 0:256], 0.0, op.add, op.subtract)
+    cc = T.k1[:, 768:1024]
+    x = None
+    for a in range(NV, 16):
+        x = s([ct, thb], T.jk1[:, 256 * a:256 * a + 256], cc, fn.Sign, bias=T.thb[:, a:a + 1], scale=-1.0, accum_out=T.acc1[:, a:a + 1])
+    cs = s([x], T.cn1[:, NV:16], T.acc1[:, NV:16], fn.Identity, scale=0.5, bias=128.0)
+    rp = v([ir], V.memset, T.rp[:, 0:2048:256], 0.0)
+    for a in range(NV):
+        x = ts([ct, thr], T.z1[:, 256 * a:256 * a + 256], cc, T.thr[:, a:a + 1], None, op.is_le)
+    x = scan([x, rp], T.zs1[:, 0:256 * NV], T.rp[:, 0:256 * NV], T.z1[:, 0:256 * NV], 0.0, op.mult, op.add)
+    cv = cp([x], T.cn1[:, 0:NV], T.zs1[:, 255:256 * NV:256])
+    l1 = cp([cv, cs], T.ll1[:, 0:16], T.cn1[:])
+    l2 = cp([], T.ll1[:, 16:32], T.cn1[:])
+    le = ts([], T.le[:], T.cn1[:], 255.5, -4096.0, op.is_ge, op.mult)
+    lt = turn([l1, l2], T.lt1[:], T.ll1[:])
+    lf = tt([le], T.lf[:], T.cn1[:], T.le[:], op.add)
+    o1 = cp([lt], T.off1[:], T.lt1[:])
+    lid = s([lf], T.lid[:], T.lf[:], fn.Relu, bias=float(256 * r + 1))
+
+    def dispatch(deps, sq, ss, lq, ls, wq_, ws_, wn_, off, sem_of):
+        pf = pick(deps, sq, ss, 64 * f0, wq_, ws_, wn_, off, 4 * f0, 64 * len(far))
+        need("g", [pf[0]])
+        send(far, lambda q: sq[:, 64 * q:64 * q + 64].bitcast(dt.uint8), lambda q: lq[:, 64 * r:64 * r + 64].bitcast(dt.uint8), sem_of)
+        pn = pick(deps, sq, ss, 64 * n0, wq_, ws_, wn_, off, 4 * n0, 64 * len(near))
+        need("g", [pn[0]])
+        send(near_to, lambda q: sq[:, 64 * q:64 * q + 64].bitcast(dt.uint8), lambda q: lq[:, 64 * r:64 * r + 64].bitcast(dt.uint8), sem_of)
+        need("g", [pf[1], pn[1]])
+        send(far + near_to, lambda q: ss[:, 64 * q:64 * q + 64], lambda q: ls[:, 64 * r:64 * r + 64], sem_of)
+
+    hf = 64 * (r % 2)
+    dl1 = dma("y", [lid], "dl1", T.lst1[:], T.lid[0:32, 0:16])
+    do1 = dma("y", [], "do1", T.ldl1[r, hf:hf + 64, 0], T.lid[4 * r:4 * r + 4, 0:16])
+    dispatch([o1, xq], T.send1, T.send1s, T.land1, T.land1s, T.xq, T.xs, 258, T.off1, lambda q: "a1")
+    own1 = pick([o1, xq], T.land1, T.land1s, 64 * r, T.xq, T.xs, 258, T.off1, 4 * r, 64)
+    need("g", [dl1])
+    send(far + near_to, lambda q: T.lst1[q // 2], lambda q: T.ldl1[r], lambda q: "l1", True)
+    arr1 = ("a1", 2 * (wf * len(far) + wn * len(near_to)))
+    lst1 = ("l1", n_ranks - 1)
+    count["a1"], count["l1"] = arr1[1], lst1[1]
+
+    c4 = ts([], T.ii[:, 4:5], p, 15, None, op.bitwise_and)
+    c3 = ts([], T.ii[:, 3:4], p, 4, 1, op.arith_shift_right, op.bitwise_and)
+    c5 = ts([], T.ii[:, 5:6], p, 4, None, op.arith_shift_right)
+    c6 = ts([], T.ii[:, 6:7], p, 7, None, op.bitwise_and)
+    c7 = ts([], T.ii[:, 7:8], p, 3, 3, op.arith_shift_right, op.bitwise_and)
+    c8 = ts([], T.ii[:, 8:9], p, 1, None, op.bitwise_and)
+    c9 = ts([], T.ii[:, 9:10], p, 1, 1, op.arith_shift_right, op.bitwise_and)
+    ua = ts([i4], T.iua[:], T.iu[:], 7, None, op.bitwise_and)
+    iz = fill(T.idw[:], 0.0)
+    jz = fill(T.iv[:], 1.0)
+    f4 = ts([c4], T.cf[:, 4:5], T.ii[:, 4:5], 4.0, None, op.mult)
+    f3 = ts([c3], T.cf[:, 3:4], T.ii[:, 3:4], 16.0, None, op.mult)
+    f5 = cp([c4], T.cf[:, 5:6], T.ii[:, 4:5])
+    f6 = ts([c4], T.cf[:, 6:7], T.ii[:, 4:5], 8.0, -1.0, op.is_ge, op.mult)
+    f7 = cp([c7], T.cf[:, 7:8], T.ii[:, 7:8])
+    f8 = ts([c6], T.cf[:, 8:9], T.ii[:, 6:7], float(WB), -1.0, op.mult, op.add)
+    f9 = cp([c9], T.cf[:, 9:10], T.ii[:, 9:10])
+    f10 = ts([c8], T.cf[:, 10:11], T.ii[:, 8:9], 32.0, None, op.mult)
+    dcol2 = ts([c6], T.dcol2[:, 0:1], T.ii[:, 6:7], 8.0, None, op.subtract)
+    fct = s([i2, f4], T.fct[:], T.ict[:], fn.Identity, bias=T.cf[:, 4:5])
+    dj = s([i7, f3], T.dj[:], T.idj[:], fn.Identity, bias=T.cf[:, 3:4])
+    tri = s([i6, f5], T.tri[:], T.itr[:], fn.Identity, bias=T.cf[:, 5:6])
+    q3 = fill(T.fp2[:, 0:30], 3.0)
+    ue = ts([ua], T.iue[:], T.iua[:], 0.0, None, op.is_equal)
+    ug = ts([i5, f7], T.iug[:], T.iuq[:], T.cf[:, 7:8], None, op.is_gt)
+    g0 = ts([c5, f9], T.fg[:, 0:1], T.ii[:, 5:6], 2.0, T.cf[:, 9:10], op.mult, op.add)
+    oct_ = cp([fct], T.offct[:], T.fct[:])
+    wvq = v([dwv], V.quantize_mx, T.wvq[:], T.wvs[:], T.wvt[:])
+    p2z = fill(T.p2t[:, 16:512], 0.0)
+    hz = fill(T.ht[:, 2048:2056], 0.0)
+    q4 = ts([q3, f6, i3], T.fp2[:, 1:30:2], T.ip2[:, 0:15], T.cf[:, 6:7], 3.0, op.mult, op.add)
+    um = tt([ue, ug], T.um[:], T.iue[:], T.iug[:], op.mult)
+    g1 = ts([g0, f10], T.fg[:, 1:2], T.fg[:, 0:1], T.cf[:, 10:11], None, op.add)
+    op2 = cp([q4], T.offp2[:, 0:30], T.fp2[:, 0:30])
+    p2r = v([dp2, p2z], V.quantize_mx, T.p2r[:], T.p2rs[:], T.p2t[:])
+    r8 = fill(T.rp8[:], 1.0)
+    og = cp([g1], T.offg[:, 0:1], T.fg[:, 1:2])
+    p2q = pick([p2r, op2], T.p2q, T.p2s, 0, T.p2r, T.p2rs, 128, T.offp2, 0, 480)
+    rp8 = v([r8], V.memset, T.rp8[:, 0:128:8], 0.0)
+    wq = v([dw], V.quantize_mx, T.wq[:], T.ws[:], T.wt[:])
+    for e in range(n_ranks):
+        wz = fill(T.wn[:, WB * e:WB * e + WL], 0.0)
+    lz = fill(T.lz[:], 0.0)
+
+    div = did0 = None
+    mine = T.ldl1[:, hf:hf + 64, 0]
+    for a in range(4):
+        div = dma("y", [lst1, do1, jz], "div", T.iv[32 * a:32 * a + 32:8, 0:128], mine)
+    for a in range(8):
+        did0 = dma("y", [iz], "did0", T.idw[16 * a:16 * a + 1, 0:512], mine)
+
+    cpk = []
+    for t in range(4):
+        a = cp([arr1, oct_, own1[0]], T.ctq[:, 128 * t:128 * t + 128].bitcast(dt.uint32), T.land1[:].bitcast(dt.uint32).indirect(T.offct[:, 8 * t:8 * t + 8]))
+        b = s([arr1, oct_, own1[1]], T.cts[:, 128 * t:128 * t + 128], T.land1s[:].indirect(T.offct[:, 8 * t:8 * t + 8]), fn.Copy)
+        cpk.append([a, b])
+
+    def c_t(t):
+        return T.ctq[:, 128 * t:128 * t + 128], T.cts[:, 128 * t:128 * t + 128]
+
+    P = [T["ps%d" % b] for b in range(8)]
+    sm = [mm(cpk[t] + [wvq, arr1], P[t][:], c_t(t)[0], c_t(t)[1], T.wvq[:], T.wvs[:]) for t in range(4)]
+    se = [None] * 4
+    for t in range(4):
+        o = T.vt[:, t:2048:4]
+        se[t] = s([sm[t]], o, P[t][:], fn.Copy) if t % 2 == 0 else cp([sm[t]], o, P[t][:])
+    vq = v(se, V.quantize_mx, T.vq[:], T.vs[:], T.vt[:])
+    aq = []
+    for h in range(2):
+        rm, re = [], []
+        for t in range(4):
+            rm.append(mm([own1[0], own1[1], arr1, se[t] if h else None], P[4 - 4 * h + t][:, 0:256], c_t(t)[0], c_t(t)[1],
+                         T.land1[:, 256 * h:256 * h + 256], T.land1s[:, 256 * h:256 * h + 256]))
+        for t in range(4):
+            b = P[4 - 4 * h + t]
+            o = T.at[:, 1024 * h + t:1024 * h + 1024:4]
+            if t < 4 - RV[h]:
+                re.append(s([rm[t]], o, b[:, 0:256], fn.Relu, scale=0.0625))
+            else:
+                re.append(ts([rm[t]], o, b[:, 0:256], 0.0, 0.0625, op.max, op.mult))
+        aq.append((v(re, V.quantize_mx, T.aq[:, 256 * h:256 * h + 256], T.asc[:, 256 * h:256 * h + 256], T.at[:, 1024 * h:1024 * h + 1024]), re))
+    om = []
+    for h in range(2):
+        om.append([mm([vq, aq[h][0]] + aq[h][1], P[4 - 4 * h + i][:, 0:256], T.vq[:, 128 * i:128 * i + 128], T.vs[:, 128 * i:128 * i + 128],
+                      T.aq[:, 256 * h:256 * h + 256], T.asc[:, 256 * h:256 * h + 256]) for i in range(4)])
+    ei = s([div], T.eb[:], T.iv[:], fn.Relu, scale=-1.0, bias=1.0)
+    he, hq, zt2 = [], [], [None] * 3
+    for h in range(2):
+        ev = []
+        for i in range(4):
+            o, b = T.ht[:, 1024 * h + i:1024 * h + 1024:4], P[4 - 4 * h + i][:, 0:256]
+            if i % 2 == 0 or i >= 2 * HV[h]:
+                ev.append(s([om[h][i]], o, b, fn.Identity, scale=0.0625))
+            else:
+                ev.append(ts([om[h][i]], o, b, 0.0625, None, op.mult))
+        he.append(ev)
+        hi = 256 if h == 0 else 514
+        hq.append(v(ev + [hz], V.quantize_mx, T.hq[:, 256 * h:hi], T.hs[:, 256 * h:hi], T.ht[:, 1024 * h:4 * hi]))
+        for b in range(3):
+            for c in (2 * h, 2 * h + 1):
+                w0 = 160 * b + 24 - 8 * c
+                zt2[b] = mm(p2q + [hq[h]] + he[0], P[4 + b][:, 0:128], T.p2q[:, w0:w0 + 128], T.p2s[:, w0:w0 + 128],
+                            T.hq[:, 128 * c:128 * c + 128], T.hs[:, 128 * c:128 * c + 128], c == 0, c == 3)
+    et = turn([ei], T.et[:], T.eb[:])
+    te = tt([et, tri], T.te[:], T.et[:, 0:128:8], T.tri[:], op.mult)
+
+    f = number(zt2, P[4:7], T.u2, T.k2, 128, T.dcol2[:, 0:1], [dcol2])
+    ff = T.k2[:, 256:384]
+    ct = scan([f, ei], T.k2[:, 384:512], ff, T.eb[:], 0.0, op.add, op.subtract)
+    x = ts([ct, um], T.bc[:], T.um[:], T.k2[:, 511:512], None, op.mult)
+    x = turn([x], T.bt[:], T.bc[:])
+    x = v([x], V.tensor_reduce, T.og[:, 0:1], T.bt[:], AxisListType.X, op.add)
+    x = ts([x, f8], T.pp[:], T.k2[:, 384:512], T.og[:, 0:1], T.cf[:, 8:9], op.add, op.add)
+    x = scan([x, f], T.pm[:], T.pp[:], ff, -100.0, op.max, op.mult)
+    x = turn([x], T.pt[:], T.pm[:])
+    x = scan([x, rp8], T.pc[:], T.rp8[:], T.pt[:], 0.0, op.mult, op.add)
+    x = tt([x, te], T.pf[:], T.pc[:, 7:128:8], T.te[:], op.max)
+    x = cp([x], T.pos[:], T.pf[:])
+    x = cp([x, dj, wz], T.wn[:].indirect(T.pos[:]), T.dj[:])
+    for e in range(n_ranks):
+        y = turn([x], T.wtr[:, WL * e:WL * e + WL], T.wn[:, WB * e:WB * e + WL])
+    x = tt([y, lz], T.lz[:, 0:16], T.wtr[:, 0:512:32], T.wtr[:, 16:512:32], op.add)
+    x = turn([x], T.lzt[:], T.lz[:])
+    xs = [s([x], T.lx[:, 32 * h + 16:32 * h + 32], T.lzt[:, 16 * h:16 * h + 16], fn.Identity, bias=512.0) for h in range(2)]
+    xv = [ts([x], T.lx[:, 32 * h:32 * h + 16], T.lzt[:, 16 * h:16 * h + 16], 512.0, None, op.add) for h in range(2)]
+    x = turn(xs + xv, T.lxt[:], T.lx[:])
+    oa = cp([x], T.off2[:, 0:32:2], T.lxt[:, 0:16])
+    o2 = cp([x], T.off2[:, 1:32:2], T.lxt[:, 32:48])
+
+    dispatch([oa, o2, hq[1]], T.send2, T.send2s, T.land2, T.land2s, T.hq, T.hs, 514, T.off2, lambda q: "a2off" if q in far else "a2on")
+    g16 = cp([og, x], T.g16[:], T.lxt[:].indirect(T.offg[:, 0:1]))
+    o3 = cp([g16], T.off3[:], T.g16[:])
+    ids = ts([o3, did0], T.idsel[:], T.idw[:].indirect(T.off3[:, 0:4]), -1.0, None, op.add)
+    dl2 = dma("y", [ids], "dl2", T.lst2[:], T.idsel[0:128:16, 0:64])
+    do2 = dma("y", [], "do2", T.ldl2[r, hf:hf + 64, 0], T.idsel[16 * r:16 * r + 1, 0:64])
+    own2 = pick([o2, hq[1]], T.land2, T.land2s, 64 * r, T.hq, T.hs, 514, T.off2, 4 * r, 64)
+    need("g", [dl2])
+    send(far + near_to, lambda q: T.lst2[q // 2], lambda q: T.ldl2[r], lambda q: "l2", True)
+    an = ("a2on", 2 * wn * len(near_to))
+    af = ("a2off", 2 * wf * len(far))
+    lst2 = ("l2", n_ranks - 1)
+    count["a2on"], count["a2off"], count["l2"] = an[1], af[1], lst2[1]
+
+    def ycols(b, c0, w, deps):
+        return mm([wq] + deps, b[:, 0:w], T.wq[:], T.ws[:], T.land2[:, c0:c0 + w], T.land2s[:, c0:c0 + w])
+
+    c0, w, dn = 64 * n0, 64 * len(near), [an, own2[0], own2[1]]
+    ym = ycols(P[7], c0, w, he[0] + dn)
+    dma("s", dn, "doc", T.oc[:, 4 * c0:4 * c0 + 4 * w], T.land2[:, c0:c0 + w].bitcast(dt.uint8))
+    ye = cp([ym], T.yt[:, c0:c0 + w], P[7][:, 0:w])
+    dma("s", [ye], "dy", T.y[:, c0:c0 + w], T.yt[:, c0:c0 + w])
+    c0, w = 64 * f0, 64 * len(far)
+    dma("s", [af], "doc", T.oc[:, 4 * c0:4 * c0 + 4 * w], T.land2[:, c0:c0 + w].bitcast(dt.uint8))
+    w //= 2
+    ym = [ycols(P[3 - k], c0 + w * k, w, he[1] + [af]) for k in range(2)]
+    ye = [cp([ym[0]], T.yt[:, c0:c0 + w], P[3][:, 0:w]), s([ym[1]], T.yt[:, c0 + w:c0 + 2 * w], P[2][:, 0:w], fn.Copy)]
+    dma("s", ye, "dy", T.y[:, c0:c0 + 2 * w], T.yt[:, c0:c0 + 2 * w])
+    for m in range(4):
+        dma("y", dn + [af], "dos", T.osc[4 * m:4 * m + 4, :], T.land2s[32 * m:32 * m + 4, :])
+    dma("y", [lst2, do2], "did", T.id[:], T.ldl2[:, hf:hf + 64, 0])
+    need("y", [(k, count[k]) for k in count])

@@ -1,49 +1,95 @@
 from concourse.bass import DstId, RemoteDMATransfer
-from concourse.mybir import dt, AluOpType, AxisListType, ActivationFunctionType
+from concourse.mybir import dt, AluOpType, ActivationFunctionType
 
-NV = 8
-RV = (1, 2)
-HV = (2, 2)
-WL, WB = 64, 512
+NV1, NV2 = 5, 10
+SV = "svsv"
+RV = ("sssv", "ssvv")
+HV = ("svsv", "svsv")
 
 BF, F4, I4, U2, CO, PL = "bfloat16", "float32", "int32", "uint16", "float8_e4m3fn_x4", "uint8"
 SCRATCH = {}
-for _n, _w, _d in (("zr", 256, BF), ("rp", 2048, BF), ("xt", 1032, BF), ("plt", 512, BF), ("p2t", 512, BF),
+for _n, _w, _d in (("zr", 128, BF), ("rp", 128 * NV2, BF), ("xt", 1032, BF), ("plt", 528, BF), ("p2t", 512, BF),
                    ("wvt", 2048, BF), ("wt", 512, BF), ("vt", 2048, BF), ("at", 2048, BF), ("ht", 2056, BF),
-                   ("yt", 512, F4), ("ii", 16, I4), ("fpl", 24, F4), ("offpl", 24, U2), ("i16", 16, F4), ("cf", 16, F4),
-                   ("thr", 16, BF), ("thb", 16, F4), ("dcol", 2, BF), ("dcol2", 2, BF), ("ict", 32, F4), ("fct", 32, F4), ("offct", 32, U2),
-                   ("ip2", 16, F4), ("fp2", 32, F4), ("offp2", 32, U2), ("iu", 32, I4), ("iua", 32, I4), ("iuq", 32, F4), ("iue", 32, F4),
-                   ("iug", 32, F4), ("um", 32, BF), ("itr", 16, F4), ("tri", 16, F4), ("idj", 256, F4), ("dj", 256, F4), ("rp8", 128, BF),
-                   ("fg", 4, F4), ("offg", 2, U2), ("ll1", 32, F4), ("lt1", 32, F4), ("off1", 32, U2), ("off2", 32, U2), ("le", 16, F4),
-                   ("lf", 16, F4), ("lid", 16, F4), ("iv", 128, F4), ("eb", 128, BF), ("et", 128, BF), ("te", 16, F4), ("idw", 520, F4),
-                   ("u1", 768, BF), ("k1", 1024, BF), ("z1", 2048, BF), ("zs1", 2048, BF), ("jk1", 4096, BF), ("acc1", 16, F4), ("cn1", 16, F4),
-                   ("u2", 384, BF), ("k2", 512, BF), ("bc", 32, BF), ("bt", 32, BF), ("og", 2, F4), ("pp", 128, F4), ("pm", 128, F4),
-                   ("pt", 128, F4), ("pc", 128, F4), ("pf", 16, F4), ("pos", 16, U2), ("wn", 8 * WB + 256, F4), ("wtr", 512, F4),
-                   ("lz", 32, F4), ("lzt", 32, F4), ("lx", 64, F4), ("lxt", 64, F4), ("g16", 16, F4), ("off3", 16, U2), ("idsel", 64, F4)):
+                   ("yt", 512, F4), ("ii", 16, I4), ("offpl", 12, U2), ("i16", 16, F4), ("cf", 16, F4),
+                   ("tha", 8, BF), ("th1", 8, BF), ("thb", 16, BF), ("th2", 16, BF), ("dcol", 2, BF), ("ict", 16, F4), ("fct", 16, F4),
+                   ("offct", 16, U2), ("off1", 32, U2), ("off2", 32, U2), ("off3", 8, U2), ("le", 16, F4), ("lf", 16, F4), ("lid", 16, F4),
+                   ("iv", 128, F4), ("eb", 128, BF), ("idw", 520, F4), ("idsel", 128, F4),
+                   ("u1", 384, BF), ("k1", 512, BF), ("z1", 128 * NV1, BF), ("zs1", 128 * NV1, BF), ("jk1", 128 * (8 - NV1), BF),
+                   ("acc1", 8, F4), ("cn1", 8, F4), ("ll1", 32, F4), ("lt1", 32, F4),
+                   ("u2", 384, BF), ("k2", 512, BF), ("z2", 128 * NV2, BF), ("zs2", 128 * NV2, BF), ("jk2", 128 * (16 - NV2), BF),
+                   ("acc2", 16, F4), ("cn2", 16, F4), ("cu2", 16, F4), ("ll2", 32, F4), ("lt2", 32, F4)):
     SCRATCH[_n] = ("sbuf", [128, _w], _d)
-for _n, _m, _w in (("xq", "xs", 258), ("plr", "plrs", 128), ("plq", "pls", 384), ("p2r", "p2rs", 128), ("p2q", "p2s", 480), ("wvq", "wvs", 512),
+for _n, _m, _w in (("xq", "xs", 258), ("plr", "plrs", 128), ("plq", "pls", 704), ("p2r", "p2rs", 128), ("p2q", "p2s", 608), ("wvq", "wvs", 512),
                    ("wq", "ws", 128), ("send1", "send1s", 512), ("land1", "land1s", 512), ("ctq", "cts", 512), ("vq", "vs", 512),
                    ("aq", "asc", 512), ("hq", "hs", 514), ("send2", "send2s", 512), ("land2", "land2s", 512)):
     SCRATCH[_n] = ("sbuf", [128, _w], CO)
     SCRATCH[_m] = ("sbuf", [128, _w], PL)
+for _n in ("hand1", "hand2"):
+    SCRATCH[_n] = ("sbuf", [128, 512], PL)
 for _n, _w in (("lst1", 4), ("ldl1", 8), ("lst2", 4), ("ldl2", 8)):
     SCRATCH[_n] = ("dram", [_w, 128, 1], F4)
 for _h in range(8):
     SCRATCH["ps%d" % _h] = ("psum", [128, 512], F4)
 SEMAPHORES = ["v", "s", "t", "gi", "dx", "dpl", "dwv", "dw", "dp2", "dl1", "do1", "div", "did0", "dl2", "do2", "did",
-              "doc", "dos", "dy", "snd", "a1", "l1", "a2on", "a2off", "l2"]
+              "doc", "dos", "dy", "snd", "a1n", "a1f", "l1", "a2n", "a2f", "l2", "h1f", "h1n", "h2f", "h2n"]
 
 
 def rank_program(g, core, T, topo):
-    r = T.rank_of(core)
-    if r is None:
-        return
     cores = T.cores
     n_ranks = len(cores)
-    Q = {"v": g.vector, "s": g.scalar, "t": g.tensor, "y": g.sync, "g": g}
-    V, S, PE = g.vector, g.scalar, g.tensor
+
+    def mates_of(q):
+        return [a for a in range(n_ranks) if topo.chip(cores[a]) == topo.chip(cores[q])]
+
+    def helper(q):
+        free = [c for c in topo.cores_of(cores[q]) if T.rank_of(c) is None and topo.die(c) != topo.die(cores[q])]
+        return free[mates_of(q).index(q)]
+
+    r = T.rank_of(core)
+    hands_on = r is None
+    if hands_on:
+        mine = [q for q in range(n_ranks) if helper(q) == core]
+        if not mine:
+            return
+        r = mine[0]
     op, fn = AluOpType, ActivationFunctionType
     waited, count = {}, {}
+
+    near = mates_of(r)
+    far = [q for q in range(n_ranks) if q not in near]
+    near_to = [near[(near.index(r) + k) % len(near)] for k in range(1, len(near))]
+    n0, f0 = min(near), min(far)
+    far_pool = topo.engines(core, cores[far[0]])
+    near_pool = [e for e in topo.engines(core, cores[near_to[0]]) if e not in far_pool]
+    wf = len(far_pool) // len(far)
+    wn = len(near_pool) // len(near)
+    eng = {}
+    for i, q in enumerate(far):
+        eng[q] = far_pool[wf * i:wf * i + wf]
+    for i, q in enumerate(near_to):
+        eng[q] = near_pool[wn * i:wn * i + wn] if i + 1 < len(near_to) else near_pool[wn * i:]
+
+    def transfer(c, engines, sem, src, dst):
+        mask = 0
+        for e in engines:
+            mask += 1 << e
+        count["snd"] = count.get("snd", 0) + len(engines)
+        rid, pid, _ = topo.addr(c)
+        return RemoteDMATransfer(dst_ids=[DstId(rid=rid, pnc=pid)], dma_engine_mask=mask, remote_sem=T.sem[sem], src=src, dst=dst)
+
+    def call(tr):
+        g.remote_dma_fused(tr, local_sem=T.sem.snd)
+
+    if hands_on:
+        for k, (hand, land) in enumerate(((T.hand1, T.land1s), (T.hand2, T.land2s))):
+            for to, x in ((far, "f"), (near_to, "n")):
+                g.wait_ge(T.sem["h%d%s" % (k + 1, x)], len(near_pool))
+                call([transfer(cores[q], eng[q], "a%d%s" % (k + 1, x), hand[:, 64 * q:64 * q + 64], land[:, 64 * r:64 * r + 64]) for q in to])
+        g.wait_ge(T.sem.snd, count["snd"])
+        return
+
+    Q = {"v": g.vector, "s": g.scalar, "t": g.tensor, "y": g.sync, "g": g}
+    V, S, PE = g.vector, g.scalar, g.tensor
 
     def need(q, deps):
         best = {}
@@ -90,8 +136,8 @@ def rank_program(g, core, T, topo):
     def cp(deps, out, in_):
         return v(deps, V.tensor_copy, out, in_)
 
-    def fill(out, c):
-        return v([], V.memset, out, c)
+    def fill(out, c, deps=()):
+        return v(list(deps), V.memset, out, c)
 
     def turn(deps, out, in_):
         return v(deps, V.transpose, out, in_)
@@ -99,36 +145,27 @@ def rank_program(g, core, T, topo):
     def scan(deps, *a):
         return v(deps, V.tensor_tensor_scan, *a)
 
-    near = [q for q in range(n_ranks) if topo.chip(cores[q]) == topo.chip(core)]
-    far = [q for q in range(n_ranks) if q not in near]
-    near_to = [q for q in near if q != r]
-    n0, f0 = min(near), min(far)
-    far_pool = topo.engines(core, cores[far[0]])
-    near_pool = [e for e in topo.engines(core, cores[near_to[0]]) if e not in far_pool]
+    def quant(deps, q, sc, tile):
+        return v(deps, V.quantize_mx, q, sc, tile)
 
-    def share(pool, k):
-        w = 1
-        while 2 * w * k <= len(pool):
-            w *= 2
-        return w
+    def pick_c(deps, dq, c0, win, off):
+        n = 16 * off[2]
+        return cp(deps, dq[:, c0:c0 + n].bitcast(dt.uint32), win.bitcast(dt.uint32).indirect(off[0][:, off[1]:off[1] + off[2]]))
 
-    wf, wn = share(far_pool, len(far)), share(near_pool, len(near_to))
-    eng = {}
-    for i, q in enumerate(far):
-        eng[q] = far_pool[wf * i:wf * i + wf]
-    for i, q in enumerate(near_to):
-        eng[q] = near_pool[wn * i:wn * i + wn]
+    def pick_s(deps, ds, c0, win, off):
+        n = 16 * off[2]
+        return s(deps, ds[:, c0:c0 + n], win.indirect(off[0][:, off[1]:off[1] + off[2]]), fn.Copy)
 
-    def send(to, src_of, dst_of, sem_of, few=False):
-        tr = []
-        for q in to:
-            mask = 0
-            for e in eng[q][0:1] if few else eng[q]:
-                mask += 1 << e
-                count["snd"] = count.get("snd", 0) + 1
-            rid, pid, _ = topo.addr(cores[q])
-            tr.append(RemoteDMATransfer(dst_ids=[DstId(rid=rid, pnc=pid)], dma_engine_mask=mask, remote_sem=T.sem[sem_of(q)], src=src_of(q), dst=dst_of(q)))
-        g.remote_dma_fused(tr, local_sem=T.sem.snd)
+    def out_of_psum(who, deps, out, ps, relu, scale):
+        if who == "s":
+            if scale is None:
+                return s(deps, out, ps, fn.Copy)
+            return s(deps, out, ps, fn.Relu if relu else fn.Identity, scale=scale)
+        if scale is None:
+            return cp(deps, out, ps)
+        if relu:
+            return ts(deps, out, ps, 0.0, scale, op.max, op.mult)
+        return ts(deps, out, ps, scale, None, op.mult)
 
     dpl = dma("s", [], "dpl", T.plt[:, 0:16], T.pl[:, 0:16])
     dx = dma("y", [], "dx", T.xt[:, 0:1024], T.x[:])
@@ -137,234 +174,199 @@ def rank_program(g, core, T, topo):
     dp2 = dma("y", [], "dp2", T.p2t[:, 0:16], T.p2[:, 0:16])
 
     i0 = io([[1, 1]], T.ii[:, 0:1], 0, 1, False)
-    ip = io([[1, 3], [0, 8]], T.fpl[:])
     i1 = io([[1, 16]], T.i16[:])
-    ir = io([[0, 2048]], T.rp[:], base=1)
-    i2 = io([[1, 4], [64, 8]], T.ict[:])
-    i3 = io([[-1, 3], [0, 5]], T.ip2[:, 0:15], base=3)
-    i4 = io([[1, 32]], T.iu[:], 128, -1, False)
-    i5 = io([[1, 4], [0, 8]], T.iuq[:])
-    i6 = io([[16, 16]], T.itr[:], base=8 * WB)
-    i7 = io([[32, 4], [128, 4], [1, 16]], T.idj[:], base=-512)
-    pz = fill(T.plt[:, 16:512], 0.0)
+    zr = io([[0, 128]], T.zr[:])
+    ir = io([[0, 128 * NV1]], T.rp[:, 0:128 * NV1], base=1)
+    i2 = io([[1, 4], [64, 4]], T.ict[:])
+    pz = fill(T.plt[:, 16:528], 0.0)
     xz = fill(T.xt[:, 1024:1032], 0.0)
+    for b in range(3):
+        opl = fill(T.offpl[:, 4 * b:4 * b + 4], b)
+    zeros = T.plt[:, 16:528]
     p = T.ii[:, 0:1]
     c1 = ts([i0], T.ii[:, 1:2], p, 31, 2, op.bitwise_and, op.arith_shift_right)
     c2 = ts([], T.ii[:, 2:3], p, 3, None, op.bitwise_and)
-    opl = cp([ip], T.offpl[:], T.fpl[:])
+    c3 = ts([], T.ii[:, 3:4], p, 5, 1, op.arith_shift_right, op.bitwise_and)
+    for b in range(4):
+        plz = quant([pz], T.plq[:, 192 * b:192 * b + 128], T.pls[:, 192 * b:192 * b + 128], zeros)
     dcol = ts([c1], T.dcol[:, 0:1], T.ii[:, 1:2], 8.0, None, op.subtract)
-    f1 = ts([c2], T.cf[:, 1:2], T.ii[:, 2:3], 16.0, None, op.mult)
-    zr = fill(T.zr[:], 0.0)
-    thr = ts([i1, f1], T.thr[:], T.i16[:], T.cf[:, 1:2], None, op.add)
-    thb = ts([i1, f1], T.thb[:], T.i16[:], T.cf[:, 1:2], 0.5, op.add, op.add)
+    f1 = ts([c2], T.cf[:, 1:2], T.ii[:, 2:3], 16.0, 0.5, op.mult, op.add)
+    f2 = ts([c3], T.cf[:, 2:3], T.ii[:, 3:4], 8.0, None, op.mult)
+    plr = quant([dpl, pz], T.plr[:], T.plrs[:], T.plt[:, 0:512])
+    tha = ts([i1, f1, f2], T.tha[:], T.i16[:, 0:8], T.cf[:, 1:2], T.cf[:, 2:3], op.add, op.add)
+    th1 = ts([], T.th1[0:64, :], T.i16[0:64, 0:8], T.cf[0:64, 1:2], T.cf[0:64, 2:3], op.add, op.add)
+    plq = [[pick_c([plr, opl], T.plq, 192 * b + 128, T.plr[:], (T.offpl, 4 * b, 4)),
+            pick_s([plr, opl], T.pls, 192 * b + 128, T.plrs[:], (T.offpl, 4 * b, 4))] for b in range(3)]
+    xq = quant([dx, xz], T.xq[:], T.xs[:], T.xt[:])
+    rp = fill(T.rp[:, 0:128 * NV1:128], 0.0, [ir])
 
-    def pick(deps, dq, ds, c0, wq_, ws_, wn_, off, e0, n):
-        e1 = e0 + n // 16
-        a = cp(deps, dq[:, c0:c0 + n].bitcast(dt.uint32), wq_[:, 0:wn_].bitcast(dt.uint32).indirect(off[:, e0:e1]))
-        b = s(deps, ds[:, c0:c0 + n], ws_[:, 0:wn_].indirect(off[:, e0:e1]), fn.Copy)
-        return [a, b]
+    P = [T["ps%d" % b] for b in range(8)]
+    zt = [None] * 3
+    for b in range(3):
+        for h in range(2):
+            w0 = 192 * b + 128 - 64 * h
+            zt[b] = mm(plq[b] + [plz, xq], P[b][:, 0:128], T.plq[:, w0:w0 + 128], T.pls[:, w0:w0 + 128],
+                       T.xq[:, 128 * h:128 * h + 128], T.xs[:, 128 * h:128 * h + 128], h == 0, h == 1)
 
-    plr = v([dpl, pz], V.quantize_mx, T.plr[:], T.plrs[:], T.plt[:])
-    plq = pick([plr, opl], T.plq, T.pls, 0, T.plr, T.plrs, 128, T.offpl, 0, 384)
-    xq = v([dx, xz], V.quantize_mx, T.xq[:], T.xs[:], T.xt[:])
-
-    zt = [mm(plq + [xq], T["ps%d" % b][:, 0:256], T.plq[:, 128 * b:128 * b + 128], T.pls[:, 128 * b:128 * b + 128], T.xq[:, 0:256], T.xs[:, 0:256]) for b in range(3)]
-
-    def number(zt, zp, u, k, w, dc, deps):
-        a, b, c = [ts([zt[i]], u[:, w * i:w * i + w], zp[i][:, 0:w], 0.0, lo, op.is_lt, m)
+    def running(zt, zp, u, k, less, deps):
+        a, b, c = [ts([zt[i]], u[:, 128 * i:128 * i + 128], zp[i][:, 0:128], 0.0, lo, op.is_lt, m)
                    for i, (lo, m) in enumerate(((-8.0, op.add), (2.0, op.mult), (4.0, op.mult)))]
-        d = scan([a, b], k[:, 0:w], u[:, w:2 * w], u[:, 0:w], -100.0, op.max, op.add)
-        e = scan([c, d], k[:, w:2 * w], u[:, 2 * w:3 * w], k[:, 0:w], -100.0, op.max, op.add)
-        return ts([e] + deps, k[:, 2 * w:3 * w], k[:, w:2 * w], dc, None, op.is_equal)
+        d = scan([a, b], k[:, 0:128], u[:, 128:256], u[:, 0:128], -100.0, op.max, op.add)
+        e = scan([c, d], k[:, 128:256], u[:, 256:384], k[:, 0:128], -100.0, op.max, op.add)
+        f = ts([e, dcol], k[:, 256:384], k[:, 128:256], T.dcol[:, 0:1], None, op.is_equal)
+        return scan([f] + deps, k[:, 384:512], k[:, 256:384], less, 0.0, op.add, op.subtract)
 
-    f = number(zt, [T.ps0, T.ps1, T.ps2], T.u1, T.k1, 256, T.dcol[:, 0:1], [dcol])
-    ct = scan([f, zr], T.k1[:, 768:1024], T.k1[:, 512:768], T.zr[:, 0:256], 0.0, op.add, op.subtract)
-    cc = T.k1[:, 768:1024]
-    x = None
-    for a in range(NV, 16):
-        x = s([ct, thb], T.jk1[:, 256 * a:256 * a + 256], cc, fn.Sign, bias=T.thb[:, a:a + 1], scale=-1.0, accum_out=T.acc1[:, a:a + 1])
-    cs = s([x], T.cn1[:, NV:16], T.acc1[:, NV:16], fn.Identity, scale=0.5, bias=128.0)
-    rp = v([ir], V.memset, T.rp[:, 0:2048:256], 0.0)
-    for a in range(NV):
-        x = ts([ct, thr], T.z1[:, 256 * a:256 * a + 256], cc, T.thr[:, a:a + 1], None, op.is_le)
-    x = scan([x, rp], T.zs1[:, 0:256 * NV], T.rp[:, 0:256 * NV], T.z1[:, 0:256 * NV], 0.0, op.mult, op.add)
-    cv = cp([x], T.cn1[:, 0:NV], T.zs1[:, 255:256 * NV:256])
-    l1 = cp([cv, cs], T.ll1[:, 0:16], T.cn1[:])
-    l2 = cp([], T.ll1[:, 16:32], T.cn1[:])
-    le = ts([], T.le[:], T.cn1[:], 255.5, -4096.0, op.is_ge, op.mult)
-    lt = turn([l1, l2], T.lt1[:], T.ll1[:])
-    lf = tt([le], T.lf[:], T.cn1[:], T.le[:], op.add)
-    o1 = cp([lt], T.off1[:], T.lt1[:])
-    lid = s([lf], T.lid[:], T.lf[:], fn.Relu, bias=float(256 * r + 1))
+    def counts(deps, cc, th, n, nv, z, zs, jk, acc, cn):
+        for a in range(nv, n):
+            x = s(deps, jk[:, 128 * (a - nv):128 * (a - nv) + 128], cc, fn.Sign, bias=th[:, a:a + 1], scale=-1.0, accum_out=acc[:, a:a + 1])
+        cs = s([x], cn[:, nv:n], acc[:, nv:n], fn.Identity, scale=0.5, bias=64.0)
+        for a in range(nv):
+            x = ts(deps, z[:, 128 * a:128 * a + 128], cc, th[:, a:a + 1], None, op.is_le)
+        return scan([x], zs[:], T.rp[:, 0:128 * nv], z[:], 0.0, op.mult, op.add), cs
 
-    def dispatch(deps, sq, ss, lq, ls, wq_, ws_, wn_, off, sem_of):
-        pf = pick(deps, sq, ss, 64 * f0, wq_, ws_, wn_, off, 4 * f0, 64 * len(far))
-        need("g", [pf[0]])
-        send(far, lambda q: sq[:, 64 * q:64 * q + 64].bitcast(dt.uint8), lambda q: lq[:, 64 * r:64 * r + 64].bitcast(dt.uint8), sem_of)
-        pn = pick(deps, sq, ss, 64 * n0, wq_, ws_, wn_, off, 4 * n0, 64 * len(near))
-        need("g", [pn[0]])
-        send(near_to, lambda q: sq[:, 64 * q:64 * q + 64].bitcast(dt.uint8), lambda q: lq[:, 64 * r:64 * r + 64].bitcast(dt.uint8), sem_of)
-        need("g", [pf[1], pn[1]])
-        send(far + near_to, lambda q: ss[:, 64 * q:64 * q + 64], lambda q: ls[:, 64 * r:64 * r + 64], sem_of)
+    def offsets(deps, ll, lt, off):
+        x = [turn(deps, lt[32 * a:32 * a + 32, :], ll[0:32, :]) for a in range(2)]
+        return x, [cp(x, off[64 * a:64 * a + 64, :], lt[0:64, :]) for a in range(2)]
+
+    ct = running(zt, P[0:3], T.u1, T.k1, T.zr[:], [zr])
+    x = ts([ct, tha], T.th1[64:128, :], T.tha[64:128, :], T.k1[0:64, 511:512], None, op.subtract)
+    cv, cs = counts([x, th1, rp], T.k1[:, 384:512], T.th1, 8, NV1, T.z1, T.zs1, T.jk1, T.acc1, T.cn1)
+    cv = cp([cv], T.cn1[:, 0:NV1], T.zs1[:, 127:128 * NV1:128])
+    ll = [tt([cv, cs], T.ll1[0:32, 16 * e + 8 * a:16 * e + 8 * a + 8], T.cn1[32 * a:32 * a + 32, :], T.cn1[64 + 32 * a:96 + 32 * a, :], op.add)
+          for e in range(2) for a in range(2)]
+    _, o1 = offsets(ll, T.ll1, T.lt1, T.off1)
+
+    def dispatch(k, deps, sq, ss, lq, hand, wq_, ws_, off, between):
+        nf, nn, hc = 4 * len(far), 4 * len(near), helper(r)
+
+        def codes(to, x):
+            return [transfer(cores[q], eng[q], "a%d%s" % (k, x), sq[:, 64 * q:64 * q + 64].bitcast(dt.uint8),
+                             lq[:, 64 * r:64 * r + 64].bitcast(dt.uint8)) for q in to]
+
+        def scales(q0, n, x):
+            return [transfer(hc, near_pool, "h%d%s" % (k, x), ss[:, 64 * q0:64 * q0 + 16 * n], hand[:, 64 * q0:64 * q0 + 16 * n])]
+
+        a, b = pick_c(deps, sq, 64 * f0, wq_, (off, 4 * f0, nf)), pick_s(deps, ss, 64 * f0, ws_, (off, 4 * f0, nf))
+        need("g", [a, b])
+        call(codes(far, "f") + scales(f0, nf, "f"))
+        between()
+        a, b = pick_c(deps, sq, 64 * n0, wq_, (off, 4 * n0, nn)), pick_s(deps, ss, 64 * n0, ws_, (off, 4 * n0, nn))
+        need("g", [b])
+        call(scales(n0, nn, "n"))
+        need("g", [a])
+        call(codes(near_to, "n"))
+        an, af = ("a%dn" % k, 2 * len(near_pool)), ("a%df" % k, 2 * len(far_pool))
+        count[an[0]], count[af[0]] = an[1], af[1]
+        return an, af
+
+    def lists(sem, src, dst):
+        call([transfer(cores[q], eng[q][0:1], sem, src[q // 2], dst[r]) for q in far + near_to])
+        count[sem] = n_ranks - 1
+        return (sem, n_ranks - 1)
 
     hf = 64 * (r % 2)
+    an, af = dispatch(1, o1 + [xq], T.send1, T.send1s, T.land1, T.hand1, T.xq[:], T.xs[:], T.off1, lambda: None)
+    le = ts(ll, T.le[0:32, :], T.ll1[0:32, 0:16], 255.5, -4096.0, op.is_ge, op.mult)
+    own = [pick_c(o1, T.land1, 64 * r, T.xq[:], (T.off1, 4 * r, 4)), pick_s(o1, T.land1s, 64 * r, T.xs[:], (T.off1, 4 * r, 4))]
+    lf = tt([le], T.lf[0:32, :], T.ll1[0:32, 0:16], T.le[0:32, :], op.add)
+    lid = s([lf], T.lid[0:32, :], T.lf[0:32, :], fn.Relu, bias=float(256 * r + 1))
     dl1 = dma("y", [lid], "dl1", T.lst1[:], T.lid[0:32, 0:16])
     do1 = dma("y", [], "do1", T.ldl1[r, hf:hf + 64, 0], T.lid[4 * r:4 * r + 4, 0:16])
-    dispatch([o1, xq], T.send1, T.send1s, T.land1, T.land1s, T.xq, T.xs, 258, T.off1, lambda q: "a1")
-    own1 = pick([o1, xq], T.land1, T.land1s, 64 * r, T.xq, T.xs, 258, T.off1, 4 * r, 64)
     need("g", [dl1])
-    send(far + near_to, lambda q: T.lst1[q // 2], lambda q: T.ldl1[r], lambda q: "l1", True)
-    arr1 = ("a1", 2 * (wf * len(far) + wn * len(near_to)))
-    lst1 = ("l1", n_ranks - 1)
-    count["a1"], count["l1"] = arr1[1], lst1[1]
+    lst1 = lists("l1", T.lst1, T.ldl1)
 
     c4 = ts([], T.ii[:, 4:5], p, 15, None, op.bitwise_and)
-    c3 = ts([], T.ii[:, 3:4], p, 4, 1, op.arith_shift_right, op.bitwise_and)
-    c5 = ts([], T.ii[:, 5:6], p, 4, None, op.arith_shift_right)
-    c6 = ts([], T.ii[:, 6:7], p, 7, None, op.bitwise_and)
-    c7 = ts([], T.ii[:, 7:8], p, 3, 3, op.arith_shift_right, op.bitwise_and)
-    c8 = ts([], T.ii[:, 8:9], p, 1, None, op.bitwise_and)
-    c9 = ts([], T.ii[:, 9:10], p, 1, 1, op.arith_shift_right, op.bitwise_and)
-    ua = ts([i4], T.iua[:], T.iu[:], 7, None, op.bitwise_and)
     iz = fill(T.idw[:], 0.0)
     jz = fill(T.iv[:], 1.0)
     f4 = ts([c4], T.cf[:, 4:5], T.ii[:, 4:5], 4.0, None, op.mult)
-    f3 = ts([c3], T.cf[:, 3:4], T.ii[:, 3:4], 16.0, None, op.mult)
-    f5 = cp([c4], T.cf[:, 5:6], T.ii[:, 4:5])
-    f6 = ts([c4], T.cf[:, 6:7], T.ii[:, 4:5], 8.0, -1.0, op.is_ge, op.mult)
-    f7 = cp([c7], T.cf[:, 7:8], T.ii[:, 7:8])
-    f8 = ts([c6], T.cf[:, 8:9], T.ii[:, 6:7], float(WB), -1.0, op.mult, op.add)
-    f9 = cp([c9], T.cf[:, 9:10], T.ii[:, 9:10])
-    f10 = ts([c8], T.cf[:, 10:11], T.ii[:, 8:9], 32.0, None, op.mult)
-    dcol2 = ts([c6], T.dcol2[:, 0:1], T.ii[:, 6:7], 8.0, None, op.subtract)
+    wvq = quant([dwv], T.wvq[:], T.wvs[:], T.wvt[:])
     fct = s([i2, f4], T.fct[:], T.ict[:], fn.Identity, bias=T.cf[:, 4:5])
-    dj = s([i7, f3], T.dj[:], T.idj[:], fn.Identity, bias=T.cf[:, 3:4])
-    tri = s([i6, f5], T.tri[:], T.itr[:], fn.Identity, bias=T.cf[:, 5:6])
-    q3 = fill(T.fp2[:, 0:30], 3.0)
-    ue = ts([ua], T.iue[:], T.iua[:], 0.0, None, op.is_equal)
-    ug = ts([i5, f7], T.iug[:], T.iuq[:], T.cf[:, 7:8], None, op.is_gt)
-    g0 = ts([c5, f9], T.fg[:, 0:1], T.ii[:, 5:6], 2.0, T.cf[:, 9:10], op.mult, op.add)
-    oct_ = cp([fct], T.offct[:], T.fct[:])
-    wvq = v([dwv], V.quantize_mx, T.wvq[:], T.wvs[:], T.wvt[:])
     p2z = fill(T.p2t[:, 16:512], 0.0)
     hz = fill(T.ht[:, 2048:2056], 0.0)
-    q4 = ts([q3, f6, i3], T.fp2[:, 1:30:2], T.ip2[:, 0:15], T.cf[:, 6:7], 3.0, op.mult, op.add)
-    um = tt([ue, ug], T.um[:], T.iue[:], T.iug[:], op.mult)
-    g1 = ts([g0, f10], T.fg[:, 1:2], T.fg[:, 0:1], T.cf[:, 10:11], None, op.add)
-    op2 = cp([q4], T.offp2[:, 0:30], T.fp2[:, 0:30])
-    p2r = v([dp2, p2z], V.quantize_mx, T.p2r[:], T.p2rs[:], T.p2t[:])
-    r8 = fill(T.rp8[:], 1.0)
-    og = cp([g1], T.offg[:, 0:1], T.fg[:, 1:2])
-    p2q = pick([p2r, op2], T.p2q, T.p2s, 0, T.p2r, T.p2rs, 128, T.offp2, 0, 480)
-    rp8 = v([r8], V.memset, T.rp8[:, 0:128:8], 0.0)
-    wq = v([dw], V.quantize_mx, T.wq[:], T.ws[:], T.wt[:])
-    for e in range(n_ranks):
-        wz = fill(T.wn[:, WB * e:WB * e + WL], 0.0)
-    lz = fill(T.lz[:], 0.0)
+    oct_ = cp([fct], T.offct[:], T.fct[:])
+    x = fill(T.rp[:, 128 * NV1:128 * NV2], 1.0)
+    thb = ts([], T.thb[:], T.i16[:], T.cf[:, 1:2], None, op.add)
+    th2 = ts([], T.th2[0:32, :], T.i16[0:32, :], T.cf[0:32, 1:2], None, op.add)
+    p2r = quant([dp2, p2z], T.p2r[:], T.p2rs[:], T.p2t[:])
+    rp2 = fill(T.rp[:, 128 * NV1:128 * NV2:128], 0.0, [x])
+    for b in range(4):
+        p2z = quant([], T.p2q[:, 160 * b:160 * b + 128], T.p2s[:, 160 * b:160 * b + 128], zeros)
+    p2q = [p2z]
+    for b in range(3):
+        p2q += [pick_c([p2r], T.p2q, 160 * b + 128, T.p2r[:], (T.offpl, 4 * b, 2)), pick_s([p2r], T.p2s, 160 * b + 128, T.p2rs[:], (T.offpl, 4 * b, 2))]
+    wq = quant([dw], T.wq[:], T.ws[:], T.wt[:])
 
     div = did0 = None
     mine = T.ldl1[:, hf:hf + 64, 0]
     for a in range(4):
-        div = dma("y", [lst1, do1, jz], "div", T.iv[32 * a:32 * a + 32:8, 0:128], mine)
-    for a in range(8):
-        did0 = dma("y", [iz], "did0", T.idw[16 * a:16 * a + 1, 0:512], mine)
+        div = dma("y", [lst1, do1, jz], "div", T.iv[a:128:32, 0:128], mine)
+    for a in range(4):
+        did0 = dma("y", [iz], "did0", T.idw[32 * a:32 * a + 1, 0:512], mine)
 
-    cpk = []
-    for t in range(4):
-        a = cp([arr1, oct_, own1[0]], T.ctq[:, 128 * t:128 * t + 128].bitcast(dt.uint32), T.land1[:].bitcast(dt.uint32).indirect(T.offct[:, 8 * t:8 * t + 8]))
-        b = s([arr1, oct_, own1[1]], T.cts[:, 128 * t:128 * t + 128], T.land1s[:].indirect(T.offct[:, 8 * t:8 * t + 8]), fn.Copy)
-        cpk.append([a, b])
+    cpk = [[], [], [], []]
+    for q0, deps in ((n0, [an] + own), (f0, [af])):
+        for t in range(4):
+            c0, lo = 128 * t + 16 * q0, 64 * q0
+            cpk[t] += [pick_c(deps + [oct_], T.ctq, c0, T.land1[:, lo:lo + 256], (T.offct, 4 * t, 4)),
+                       pick_s(deps + [oct_], T.cts, c0, T.land1s[:, lo:lo + 256], (T.offct, 4 * t, 4))]
 
     def c_t(t):
         return T.ctq[:, 128 * t:128 * t + 128], T.cts[:, 128 * t:128 * t + 128]
 
-    P = [T["ps%d" % b] for b in range(8)]
-    sm = [mm(cpk[t] + [wvq, arr1], P[t][:], c_t(t)[0], c_t(t)[1], T.wvq[:], T.wvs[:]) for t in range(4)]
-    se = [None] * 4
-    for t in range(4):
-        o = T.vt[:, t:2048:4]
-        se[t] = s([sm[t]], o, P[t][:], fn.Copy) if t % 2 == 0 else cp([sm[t]], o, P[t][:])
-    vq = v(se, V.quantize_mx, T.vq[:], T.vs[:], T.vt[:])
+    sm = [mm(cpk[t] + [wvq, an, af], P[t][:], c_t(t)[0], c_t(t)[1], T.wvq[:], T.wvs[:]) for t in range(4)]
+    se = [out_of_psum(SV[t], [sm[t]], T.vt[:, t:2048:4], P[t][:], False, None) for t in range(4)]
+    vq = quant(se, T.vq[:], T.vs[:], T.vt[:])
     aq = []
     for h in range(2):
-        rm, re = [], []
-        for t in range(4):
-            rm.append(mm([own1[0], own1[1], arr1, se[t] if h else None], P[4 - 4 * h + t][:, 0:256], c_t(t)[0], c_t(t)[1],
-                         T.land1[:, 256 * h:256 * h + 256], T.land1s[:, 256 * h:256 * h + 256]))
-        for t in range(4):
-            b = P[4 - 4 * h + t]
-            o = T.at[:, 1024 * h + t:1024 * h + 1024:4]
-            if t < 4 - RV[h]:
-                re.append(s([rm[t]], o, b[:, 0:256], fn.Relu, scale=0.0625))
-            else:
-                re.append(ts([rm[t]], o, b[:, 0:256], 0.0, 0.0625, op.max, op.mult))
-        aq.append((v(re, V.quantize_mx, T.aq[:, 256 * h:256 * h + 256], T.asc[:, 256 * h:256 * h + 256], T.at[:, 1024 * h:1024 * h + 1024]), re))
+        rm = [mm(own + [se[t] if h else None], P[4 - 4 * h + t][:, 0:256], c_t(t)[0], c_t(t)[1],
+                 T.land1[:, 256 * h:256 * h + 256], T.land1s[:, 256 * h:256 * h + 256]) for t in range(4)]
+        re = [out_of_psum(RV[h][t], [rm[t]], T.at[:, 1024 * h + t:1024 * h + 1024:4], P[4 - 4 * h + t][:, 0:256], True, 0.0625) for t in range(4)]
+        aq.append((quant(re, T.aq[:, 256 * h:256 * h + 256], T.asc[:, 256 * h:256 * h + 256], T.at[:, 1024 * h:1024 * h + 1024]), re))
     om = []
     for h in range(2):
         om.append([mm([vq, aq[h][0]] + aq[h][1], P[4 - 4 * h + i][:, 0:256], T.vq[:, 128 * i:128 * i + 128], T.vs[:, 128 * i:128 * i + 128],
                       T.aq[:, 256 * h:256 * h + 256], T.asc[:, 256 * h:256 * h + 256]) for i in range(4)])
-    ei = s([div], T.eb[:], T.iv[:], fn.Relu, scale=-1.0, bias=1.0)
     he, hq, zt2 = [], [], [None] * 3
     for h in range(2):
-        ev = []
-        for i in range(4):
-            o, b = T.ht[:, 1024 * h + i:1024 * h + 1024:4], P[4 - 4 * h + i][:, 0:256]
-            if i % 2 == 0 or i >= 2 * HV[h]:
-                ev.append(s([om[h][i]], o, b, fn.Identity, scale=0.0625))
-            else:
-                ev.append(ts([om[h][i]], o, b, 0.0625, None, op.mult))
+        ev = [out_of_psum(HV[h][i], [om[h][i]], T.ht[:, 1024 * h + i:1024 * h + 1024:4], P[4 - 4 * h + i][:, 0:256], False, 0.0625) for i in range(4)]
         he.append(ev)
         hi = 256 if h == 0 else 514
-        hq.append(v(ev + [hz], V.quantize_mx, T.hq[:, 256 * h:hi], T.hs[:, 256 * h:hi], T.ht[:, 1024 * h:4 * hi]))
+        hq.append(quant(ev + [hz], T.hq[:, 256 * h:hi], T.hs[:, 256 * h:hi], T.ht[:, 1024 * h:4 * hi]))
         for b in range(3):
             for c in (2 * h, 2 * h + 1):
-                w0 = 160 * b + 24 - 8 * c
+                w0 = 160 * b + 128 - 32 * c
                 zt2[b] = mm(p2q + [hq[h]] + he[0], P[4 + b][:, 0:128], T.p2q[:, w0:w0 + 128], T.p2s[:, w0:w0 + 128],
                             T.hq[:, 128 * c:128 * c + 128], T.hs[:, 128 * c:128 * c + 128], c == 0, c == 3)
-    et = turn([ei], T.et[:], T.eb[:])
-    te = tt([et, tri], T.te[:], T.et[:, 0:128:8], T.tri[:], op.mult)
+    ei = s([div], T.eb[:], T.iv[:], fn.Relu, scale=-1.0, bias=1.0)
 
-    f = number(zt2, P[4:7], T.u2, T.k2, 128, T.dcol2[:, 0:1], [dcol2])
-    ff = T.k2[:, 256:384]
-    ct = scan([f, ei], T.k2[:, 384:512], ff, T.eb[:], 0.0, op.add, op.subtract)
-    x = ts([ct, um], T.bc[:], T.um[:], T.k2[:, 511:512], None, op.mult)
-    x = turn([x], T.bt[:], T.bc[:])
-    x = v([x], V.tensor_reduce, T.og[:, 0:1], T.bt[:], AxisListType.X, op.add)
-    x = ts([x, f8], T.pp[:], T.k2[:, 384:512], T.og[:, 0:1], T.cf[:, 8:9], op.add, op.add)
-    x = scan([x, f], T.pm[:], T.pp[:], ff, -100.0, op.max, op.mult)
-    x = turn([x], T.pt[:], T.pm[:])
-    x = scan([x, rp8], T.pc[:], T.rp8[:], T.pt[:], 0.0, op.mult, op.add)
-    x = tt([x, te], T.pf[:], T.pc[:, 7:128:8], T.te[:], op.max)
-    x = cp([x], T.pos[:], T.pf[:])
-    x = cp([x, dj, wz], T.wn[:].indirect(T.pos[:]), T.dj[:])
-    for e in range(n_ranks):
-        y = turn([x], T.wtr[:, WL * e:WL * e + WL], T.wn[:, WB * e:WB * e + WL])
-    x = tt([y, lz], T.lz[:, 0:16], T.wtr[:, 0:512:32], T.wtr[:, 16:512:32], op.add)
-    x = turn([x], T.lzt[:], T.lz[:])
-    xs = [s([x], T.lx[:, 32 * h + 16:32 * h + 32], T.lzt[:, 16 * h:16 * h + 16], fn.Identity, bias=512.0) for h in range(2)]
-    xv = [ts([x], T.lx[:, 32 * h:32 * h + 16], T.lzt[:, 16 * h:16 * h + 16], 512.0, None, op.add) for h in range(2)]
-    x = turn(xs + xv, T.lxt[:], T.lx[:])
-    oa = cp([x], T.off2[:, 0:32:2], T.lxt[:, 0:16])
-    o2 = cp([x], T.off2[:, 1:32:2], T.lxt[:, 32:48])
+    ct = running(zt2, P[4:7], T.u2, T.k2, T.eb[:], [ei])
+    last = T.k2[:, 511:512]
+    x2 = ts([ct, thb], T.th2[64:96, :], T.thb[64:96, :], T.k2[0:32, 511:512], T.k2[32:64, 511:512], op.subtract, op.subtract)
+    x1 = ts([], T.th2[32:64, :], T.thb[32:64, :], T.k2[0:32, 511:512], None, op.subtract)
+    x3 = ts([x2], T.th2[96:128, :], T.th2[64:96, :], T.k2[64:96, 511:512], None, op.subtract)
+    cv, cs = counts([x1, x3, th2, rp2], T.k2[:, 384:512], T.th2, 16, NV2, T.z2, T.zs2, T.jk2, T.acc2, T.cn2)
+    x1 = tt([cv], T.cu2[0:64, 0:NV2], T.zs2[0:64, 127:128 * NV2:128], T.zs2[64:128, 127:128 * NV2:128], op.add)
+    x2 = tt([cs], T.cu2[0:64, NV2:16], T.cn2[0:64, NV2:16], T.cn2[64:128, NV2:16], op.add)
+    ll = [tt([x1, x2], T.ll2[0:32, 16 * e:16 * e + 16], T.cu2[0:32, :], T.cu2[32:64, :], op.add) for e in range(2)]
+    lt, o2 = offsets(ll, T.ll2, T.lt2, T.off2)
 
-    dispatch([oa, o2, hq[1]], T.send2, T.send2s, T.land2, T.land2s, T.hq, T.hs, 514, T.off2, lambda q: "a2off" if q in far else "a2on")
-    g16 = cp([og, x], T.g16[:], T.lxt[:].indirect(T.offg[:, 0:1]))
-    o3 = cp([g16], T.off3[:], T.g16[:])
-    ids = ts([o3, did0], T.idsel[:], T.idw[:].indirect(T.off3[:, 0:4]), -1.0, None, op.add)
-    dl2 = dma("y", [ids], "dl2", T.lst2[:], T.idsel[0:128:16, 0:64])
-    do2 = dma("y", [], "do2", T.ldl2[r, hf:hf + 64, 0], T.idsel[16 * r:16 * r + 1, 0:64])
-    own2 = pick([o2, hq[1]], T.land2, T.land2s, 64 * r, T.hq, T.hs, 514, T.off2, 4 * r, 64)
-    need("g", [dl2])
-    send(far + near_to, lambda q: T.lst2[q // 2], lambda q: T.ldl2[r], lambda q: "l2", True)
-    an = ("a2on", 2 * wn * len(near_to))
-    af = ("a2off", 2 * wf * len(far))
-    lst2 = ("l2", n_ranks - 1)
-    count["a2on"], count["a2off"], count["l2"] = an[1], af[1], lst2[1]
+    dl = []
+
+    def numbers():
+        o3 = [cp(lt, T.off3[32 * a:32 * a + 32, :], T.lt2[0:32, 8 * a:8 * a + 8]) for a in range(4)]
+        ids = s(o3 + [did0], T.idsel[:], T.idw[:].indirect(T.off3[:]), fn.Identity, bias=-1.0)
+        dl.append(dma("y", [ids], "dl2", T.lst2[:], T.idsel[0:128:32, :]))
+        dl.append(dma("y", [], "do2", T.ldl2[r, hf:hf + 64, 0], T.idsel[32 * (r // 2):32 * (r // 2) + 1, hf:hf + 64]))
+
+    an, af = dispatch(2, o2 + [hq[1]], T.send2, T.send2s, T.land2, T.hand2, T.hq[:], T.hs[:], T.off2, numbers)
+    own = [pick_c(o2, T.land2, 64 * r, T.hq[:], (T.off2, 4 * r, 4)), pick_s(o2, T.land2s, 64 * r, T.hs[:], (T.off2, 4 * r, 4))]
+    need("g", [dl[0]])
+    lst2 = lists("l2", T.lst2, T.ldl2)
 
     def ycols(b, c0, w, deps):
         return mm([wq] + deps, b[:, 0:w], T.wq[:], T.ws[:], T.land2[:, c0:c0 + w], T.land2s[:, c0:c0 + w])
 
-    c0, w, dn = 64 * n0, 64 * len(near), [an, own2[0], own2[1]]
+    c0, w, dn = 64 * n0, 64 * len(near), [an] + own
     ym = ycols(P[7], c0, w, he[0] + dn)
     dma("s", dn, "doc", T.oc[:, 4 * c0:4 * c0 + 4 * w], T.land2[:, c0:c0 + w].bitcast(dt.uint8))
     ye = cp([ym], T.yt[:, c0:c0 + w], P[7][:, 0:w])
@@ -377,5 +379,5 @@ def rank_program(g, core, T, topo):
     dma("s", ye, "dy", T.y[:, c0:c0 + 2 * w], T.yt[:, c0:c0 + 2 * w])
     for m in range(4):
         dma("y", dn + [af], "dos", T.osc[4 * m:4 * m + 4, :], T.land2s[32 * m:32 * m + 4, :])
-    dma("y", [lst2, do2], "did", T.id[:], T.ldl2[:, hf:hf + 64, 0])
+    dma("y", [lst2, dl[1]], "did", T.id[:], T.ldl2[:, hf:hf + 64, 0])
     need("y", [(k, count[k]) for k in count])

@@ -1,73 +1,82 @@
 from concourse.bass import DstId, RemoteDMATransfer
 from concourse.mybir import dt, AluOpType, ActivationFunctionType
 
-NV1, NV2 = 5, 10
-SV = "svsv"
-RV = ("sssv", "ssvv")
-HV = ("svsv", "svsv")
+N_CORES = 64
+NR = 2
+NV1, NV2 = 6, 11
+ORDER = [x for t in range(4) for x in (("R", 0, t), ("S", 0, t))] + [(k, h, t) for k, h in (("S", 1), ("R", 1), ("O", 0), ("O", 1)) for t in range(4)]
+WHO = "vsvsvsvssvsvsssvsvsvsssv"
+LATE = {("S", 0): 11}
+LAST_TWO = ((0, 0), (0, 1), (1, 0), (1, 1), (0, 2), (1, 2))
 
-BF, F4, I4, U2, CO, PL = "bfloat16", "float32", "int32", "uint16", "float8_e4m3fn_x4", "uint8"
+BF, H2, F4, I4, U2, CO, PL = "bfloat16", "float16", "float32", "int32", "uint16", "float8_e4m3fn_x4", "uint8"
 SCRATCH = {}
-for _n, _w, _d in (("zr", 128, BF), ("rp", 128 * NV2, BF), ("xt", 1032, BF), ("plt", 528, BF), ("p2t", 512, BF),
+for _n, _w, _d in (("zr", 128, BF), ("xt", 1032, BF), ("plt", 528, BF), ("p2t", 512, BF),
                    ("wvt", 2048, BF), ("wt", 512, BF), ("vt", 2048, BF), ("at", 2048, BF), ("ht", 2056, BF),
-                   ("yt", 512, F4), ("ii", 16, I4), ("offpl", 12, U2), ("i16", 16, F4), ("cf", 16, F4),
+                   ("yt", 512, F4), ("ii", 16, I4), ("offpl", 12, U2), ("i16", 16, F4), ("i8", 8, F4), ("cf", 16, F4),
                    ("tha", 8, BF), ("th1", 8, BF), ("thb", 16, BF), ("th2", 16, BF), ("dcol", 2, BF), ("ict", 16, F4), ("fct", 16, F4),
-                   ("offct", 16, U2), ("off1", 32, U2), ("off2", 32, U2), ("off3", 8, U2), ("le", 16, F4), ("lf", 16, F4), ("lid", 16, F4),
-                   ("iv", 128, F4), ("eb", 128, BF), ("idw", 520, F4), ("idsel", 128, F4),
-                   ("u1", 384, BF), ("k1", 512, BF), ("z1", 128 * NV1, BF), ("zs1", 128 * NV1, BF), ("jk1", 128 * (8 - NV1), BF),
-                   ("acc1", 8, F4), ("cn1", 8, F4), ("ll1", 32, F4), ("lt1", 32, F4),
-                   ("u2", 384, BF), ("k2", 512, BF), ("z2", 128 * NV2, BF), ("zs2", 128 * NV2, BF), ("jk2", 128 * (16 - NV2), BF),
+                   ("offct", 16, U2), ("off1", 32, U2), ("off2", 32, U2), ("off3", 16, U2), ("le", 16, F4), ("lf", 16, F4), ("lid", 16, F4),
+                   ("iv", 128, F4), ("eb", 128, BF), ("idw", 520, F4), ("idsel", 256, F4),
+                   ("u1", 384, BF), ("k1", 512, BF), ("zs1", 2 + 64 * NV1, H2), ("jk1", 128 * (8 - NV1), BF),
+                   ("acc1", 8, F4), ("cn1", 16, F4), ("ll1", 32, F4), ("lt1", 32, F4),
+                   ("u2", 384, BF), ("k2", 512, BF), ("zs2", 2 + 64 * NV2, H2), ("jk2", 128 * (16 - NV2), BF),
                    ("acc2", 16, F4), ("cn2", 16, F4), ("cu2", 16, F4), ("ll2", 32, F4), ("lt2", 32, F4)):
     SCRATCH[_n] = ("sbuf", [128, _w], _d)
+SCRATCH["z1"] = ("sbuf", [128, 2, 2 + 64 * NV1], BF)
+SCRATCH["z2"] = ("sbuf", [128, 2, 2 + 64 * NV2], BF)
 for _n, _m, _w in (("xq", "xs", 258), ("plr", "plrs", 128), ("plq", "pls", 704), ("p2r", "p2rs", 128), ("p2q", "p2s", 608), ("wvq", "wvs", 512),
                    ("wq", "ws", 128), ("send1", "send1s", 512), ("land1", "land1s", 512), ("ctq", "cts", 512), ("vq", "vs", 512),
-                   ("aq", "asc", 512), ("hq", "hs", 514), ("send2", "send2s", 512), ("land2", "land2s", 512)):
+                   ("aq", "asc", 512), ("hq", "hs", 514), ("send2", "send2s", 512), ("land2", "land2s", 512),
+                   ("pass1", "hand1", 256), ("pass2", "hand2", 256)):
     SCRATCH[_n] = ("sbuf", [128, _w], CO)
     SCRATCH[_m] = ("sbuf", [128, _w], PL)
-for _n in ("hand1", "hand2"):
-    SCRATCH[_n] = ("sbuf", [128, 512], PL)
 for _n, _w in (("lst1", 4), ("ldl1", 8), ("lst2", 4), ("ldl2", 8)):
     SCRATCH[_n] = ("dram", [_w, 128, 1], F4)
 for _h in range(8):
     SCRATCH["ps%d" % _h] = ("psum", [128, 512], F4)
 SEMAPHORES = ["v", "s", "t", "gi", "dx", "dpl", "dwv", "dw", "dp2", "dl1", "do1", "div", "did0", "dl2", "do2", "did",
-              "doc", "dos", "dy", "snd", "a1n", "a1f", "l1", "a2n", "a2f", "l2", "h1f", "h1n", "h2f", "h2n"]
+              "doc", "dos", "dy", "snd", "l1", "l2", "h1", "h2", "c1n", "c1f", "s1n", "s1f", "c2n", "c2f", "s2n", "s2f"]
 
 
 def rank_program(g, core, T, topo):
     cores = T.cores
     n_ranks = len(cores)
 
-    def mates_of(q):
+    def near_of(q):
         return [a for a in range(n_ranks) if topo.chip(cores[a]) == topo.chip(cores[q])]
+
+    def far_of(q):
+        return [a for a in range(n_ranks) if a not in near_of(q)]
 
     def helper(q):
         free = [c for c in topo.cores_of(cores[q]) if T.rank_of(c) is None and topo.die(c) != topo.die(cores[q])]
-        return free[mates_of(q).index(q)]
+        return free[near_of(q).index(q)]
 
-    r = T.rank_of(core)
-    hands_on = r is None
-    if hands_on:
-        mine = [q for q in range(n_ranks) if helper(q) == core]
-        if not mine:
-            return
-        r = mine[0]
-    op, fn = AluOpType, ActivationFunctionType
+    def relay(q):
+        can = [c for c in range(N_CORES) if topo.mates(topo.chip(c), topo.chip(cores[q])) and topo.may_write(c, cores[q])]
+        i = near_of(q).index(q)
+        return [c for c in can if (topo.die(c) == topo.die(cores[q])) == (i % 2 == 1)][i // 2]
+
+    def able(q):
+        return topo.may_write(cores[q], relay(far_of(q)[0]))
+
+    def halves(q):
+        far = far_of(q)
+        k, w = [a for a in near_of(q) if able(a) == able(q)].index(q) % 2, len(far) // 2
+        return far[w * k:w * k + w], far[w - w * k:2 * w - w * k]
+
+    def around(q):
+        return halves(q)[0][0:NR] if able(q) else []
+
+    def pools(c, q):
+        out = topo.engines(c, cores[far_of(q)[0]])
+        return out, [e for e in topo.engines(c, [a for a in topo.cores_of(c) if a != c][0]) if e not in out]
+
+    def deal(pool, to):
+        w = len(pool) // len(to)
+        return {q: pool[w * i:w * i + w] for i, q in enumerate(to)}
+
     waited, count = {}, {}
-
-    near = mates_of(r)
-    far = [q for q in range(n_ranks) if q not in near]
-    near_to = [near[(near.index(r) + k) % len(near)] for k in range(1, len(near))]
-    n0, f0 = min(near), min(far)
-    far_pool = topo.engines(core, cores[far[0]])
-    near_pool = [e for e in topo.engines(core, cores[near_to[0]]) if e not in far_pool]
-    wf = len(far_pool) // len(far)
-    wn = len(near_pool) // len(near)
-    eng = {}
-    for i, q in enumerate(far):
-        eng[q] = far_pool[wf * i:wf * i + wf]
-    for i, q in enumerate(near_to):
-        eng[q] = near_pool[wn * i:wn * i + wn] if i + 1 < len(near_to) else near_pool[wn * i:]
 
     def transfer(c, engines, sem, src, dst):
         mask = 0
@@ -80,13 +89,42 @@ def rank_program(g, core, T, topo):
     def call(tr):
         g.remote_dma_fused(tr, local_sem=T.sem.snd)
 
-    if hands_on:
-        for k, (hand, land) in enumerate(((T.hand1, T.land1s), (T.hand2, T.land2s))):
-            for to, x in ((far, "f"), (near_to, "n")):
-                g.wait_ge(T.sem["h%d%s" % (k + 1, x)], len(near_pool))
-                call([transfer(cores[q], eng[q], "a%d%s" % (k + 1, x), hand[:, 64 * q:64 * q + 64], land[:, 64 * r:64 * r + 64]) for q in to])
-        g.wait_ge(T.sem.snd, count["snd"])
+    r = T.rank_of(core)
+    if r is None:
+        for q in range(n_ranks):
+            if helper(q) == core:
+                out, inside = pools(core, q)
+                eng = deal(out, far_of(q))
+                for k, (hand, land) in enumerate(((T.hand1, T.land1s), (T.hand2, T.land2s))):
+                    g.wait_ge(T.sem["h%d" % (k + 1)], len(inside))
+                    call([transfer(cores[e], eng[e], "s%df" % (k + 1), hand[:, 64 * i:64 * i + 64], land[:, 64 * q:64 * q + 64])
+                          for i, e in enumerate(far_of(q))])
+                g.wait_ge(T.sem.snd, count["snd"])
+            senders = [a for a in far_of(q) if q in around(a)]
+            if relay(q) == core and senders:
+                out, lo = topo.engines(core, cores[q]), 64 * senders[0]
+                for k, (buf, land) in enumerate(((T.pass1, T.land1), (T.pass2, T.land2))):
+                    g.wait_ge(T.sem["h%d" % (k + 1)], len(out))
+                    call([transfer(cores[q], out, "c%df" % (k + 1), buf[:, 0:64].bitcast(dt.uint8), land[:, lo:lo + 64].bitcast(dt.uint8))])
+                g.wait_ge(T.sem.snd, count["snd"])
         return
+
+    op, fn = AluOpType, ActivationFunctionType
+    near, far = near_of(r), far_of(r)
+    near_to = [near[(near.index(r) + k) % len(near)] for k in range(1, len(near))]
+    n0, f0 = min(near), min(far)
+    far_pool, near_pool = pools(core, r)
+    wn = len(near_pool) // len(near)
+    first, second = halves(r)
+    eng, one = {**deal(far_pool, first), **deal(far_pool, second)}, deal(far_pool, far)
+    eng_s = deal(far_pool, near_to[:-1])
+    for i, q in enumerate(near_to):
+        eng[q] = one[q] = near_pool[wn * i:wn * i + wn] if q in eng_s else near_pool[wn * i:]
+    eng_s[near_to[-1]] = eng[near_to[-1]]
+    if able(r):
+        eng.update({q: far_pool for q in first})
+    n_cf = sum(len(far_pool) if able(a) and r in halves(a)[0] else len(far_pool) // 2 for a in far)
+    n_sn = sum(len(eng_s[q]) for q in near_to)
 
     Q = {"v": g.vector, "s": g.scalar, "t": g.tensor, "y": g.sync, "g": g}
     V, S, PE = g.vector, g.scalar, g.tensor
@@ -167,16 +205,15 @@ def rank_program(g, core, T, topo):
             return ts(deps, out, ps, 0.0, scale, op.max, op.mult)
         return ts(deps, out, ps, scale, None, op.mult)
 
-    dpl = dma("s", [], "dpl", T.plt[:, 0:16], T.pl[:, 0:16])
+    dpl = dma("y", [], "dpl", T.plt[:, 0:16], T.pl[:, 0:16])
     dx = dma("y", [], "dx", T.xt[:, 0:1024], T.x[:])
-    dwv = dma("y", [dx], "dwv", T.wvt[:], T.wv[:])
-    dw = dma("y", [], "dw", T.wt[:], T.w[:])
+    dwv = dma("y", [dpl], "dwv", T.wvt[:], T.wv[:])
     dp2 = dma("y", [], "dp2", T.p2t[:, 0:16], T.p2[:, 0:16])
 
     i0 = io([[1, 1]], T.ii[:, 0:1], 0, 1, False)
-    i1 = io([[1, 16]], T.i16[:])
+    i1 = io([[2, 8]], T.i8[:])
     zr = io([[0, 128]], T.zr[:])
-    ir = io([[0, 128 * NV1]], T.rp[:, 0:128 * NV1], base=1)
+    i3 = io([[1, 16]], T.i16[:])
     i2 = io([[1, 4], [64, 4]], T.ict[:])
     pz = fill(T.plt[:, 16:528], 0.0)
     xz = fill(T.xt[:, 1024:1032], 0.0)
@@ -189,24 +226,23 @@ def rank_program(g, core, T, topo):
     c3 = ts([], T.ii[:, 3:4], p, 5, 1, op.arith_shift_right, op.bitwise_and)
     for b in range(4):
         plz = quant([pz], T.plq[:, 192 * b:192 * b + 128], T.pls[:, 192 * b:192 * b + 128], zeros)
-    dcol = ts([c1], T.dcol[:, 0:1], T.ii[:, 1:2], 8.0, None, op.subtract)
     f1 = ts([c2], T.cf[:, 1:2], T.ii[:, 2:3], 16.0, 0.5, op.mult, op.add)
-    f2 = ts([c3], T.cf[:, 2:3], T.ii[:, 3:4], 8.0, None, op.mult)
+    f2 = cp([c3], T.cf[:, 2:3], T.ii[:, 3:4])
+    z0 = fill(T.z1[:, :, 0:2], 0.0)
     plr = quant([dpl, pz], T.plr[:], T.plrs[:], T.plt[:, 0:512])
-    tha = ts([i1, f1, f2], T.tha[:], T.i16[:, 0:8], T.cf[:, 1:2], T.cf[:, 2:3], op.add, op.add)
-    th1 = ts([], T.th1[0:64, :], T.i16[0:64, 0:8], T.cf[0:64, 1:2], T.cf[0:64, 2:3], op.add, op.add)
+    dcol = ts([c1], T.dcol[:, 0:1], T.ii[:, 1:2], 8.0, None, op.subtract)
     plq = [[pick_c([plr, opl], T.plq, 192 * b + 128, T.plr[:], (T.offpl, 4 * b, 4)),
             pick_s([plr, opl], T.pls, 192 * b + 128, T.plrs[:], (T.offpl, 4 * b, 4))] for b in range(3)]
-    xq = quant([dx, xz], T.xq[:], T.xs[:], T.xt[:])
-    rp = fill(T.rp[:, 0:128 * NV1:128], 0.0, [ir])
+    xq = [quant([dx], T.xq[:, 0:128], T.xs[:, 0:128], T.xt[:, 0:512]), quant([xz], T.xq[:, 128:258], T.xs[:, 128:258], T.xt[:, 512:1032])]
+    tha = ts([i1, f1, f2], T.tha[:], T.i8[:], T.cf[:, 1:2], T.cf[:, 2:3], op.add, op.add)
+    th1 = ts([], T.th1[0:64, :], T.i8[0:64, :], T.cf[0:64, 1:2], T.cf[0:64, 2:3], op.add, op.add)
 
     P = [T["ps%d" % b] for b in range(8)]
     zt = [None] * 3
-    for b in range(3):
-        for h in range(2):
-            w0 = 192 * b + 128 - 64 * h
-            zt[b] = mm(plq[b] + [plz, xq], P[b][:, 0:128], T.plq[:, w0:w0 + 128], T.pls[:, w0:w0 + 128],
-                       T.xq[:, 128 * h:128 * h + 128], T.xs[:, 128 * h:128 * h + 128], h == 0, h == 1)
+    for h, b in LAST_TWO:
+        w0 = 192 * b + 128 - 64 * h
+        zt[b] = mm(plq[b] + [plz, xq[h]], P[b][:, 0:128], T.plq[:, w0:w0 + 128], T.pls[:, w0:w0 + 128],
+                   T.xq[:, 128 * h:128 * h + 128], T.xs[:, 128 * h:128 * h + 128], h == 0, h == 1)
 
     def running(zt, zp, u, k, less, deps):
         a, b, c = [ts([zt[i]], u[:, 128 * i:128 * i + 128], zp[i][:, 0:128], 0.0, lo, op.is_lt, m)
@@ -216,13 +252,14 @@ def rank_program(g, core, T, topo):
         f = ts([e, dcol], k[:, 256:384], k[:, 128:256], T.dcol[:, 0:1], None, op.is_equal)
         return scan([f] + deps, k[:, 384:512], k[:, 256:384], less, 0.0, op.add, op.subtract)
 
-    def counts(deps, cc, th, n, nv, z, zs, jk, acc, cn):
+    def counts(deps, cc, th, n, nv, z, zs, jk, acc, cn, copies):
         for a in range(nv, n):
             x = s(deps, jk[:, 128 * (a - nv):128 * (a - nv) + 128], cc, fn.Sign, bias=th[:, a:a + 1], scale=-1.0, accum_out=acc[:, a:a + 1])
-        cs = s([x], cn[:, nv:n], acc[:, nv:n], fn.Identity, scale=0.5, bias=64.0)
+        cs = [s([x], cn[:, n * e + nv:n * e + n], acc[:, nv:n], fn.Identity, scale=0.5, bias=64.0) for e in range(copies)]
         for a in range(nv):
-            x = ts(deps, z[:, 128 * a:128 * a + 128], cc, th[:, a:a + 1], None, op.is_le)
-        return scan([x], zs[:], T.rp[:, 0:128 * nv], z[:], 0.0, op.mult, op.add), cs
+            x = ts(deps, z[:, :, 2 + 64 * a:66 + 64 * a], cc, th[:, a:a + 1], None, op.is_le)
+        x = scan([x], zs[:], z[:, 0, :], z[:, 1, :], 0.0, op.add, op.add)
+        return cs + [tt([x], cn[:, n * e:n * e + nv], zs[:, 65:2 + 64 * nv:64], zs[:, 1:64 * nv - 62:64], op.subtract) for e in range(copies)]
 
     def offsets(deps, ll, lt, off):
         x = [turn(deps, lt[32 * a:32 * a + 32, :], ll[0:32, :]) for a in range(2)]
@@ -230,42 +267,55 @@ def rank_program(g, core, T, topo):
 
     ct = running(zt, P[0:3], T.u1, T.k1, T.zr[:], [zr])
     x = ts([ct, tha], T.th1[64:128, :], T.tha[64:128, :], T.k1[0:64, 511:512], None, op.subtract)
-    cv, cs = counts([x, th1, rp], T.k1[:, 384:512], T.th1, 8, NV1, T.z1, T.zs1, T.jk1, T.acc1, T.cn1)
-    cv = cp([cv], T.cn1[:, 0:NV1], T.zs1[:, 127:128 * NV1:128])
-    ll = [tt([cv, cs], T.ll1[0:32, 16 * e + 8 * a:16 * e + 8 * a + 8], T.cn1[32 * a:32 * a + 32, :], T.cn1[64 + 32 * a:96 + 32 * a, :], op.add)
-          for e in range(2) for a in range(2)]
+    cn = counts([x, th1, z0], T.k1[:, 384:512], T.th1, 8, NV1, T.z1, T.zs1, T.jk1, T.acc1, T.cn1, 2)
+    ll = [tt(cn, T.ll1[0:32, a:32:2], T.cn1[32 * a:32 * a + 32, :], T.cn1[64 + 32 * a:96 + 32 * a, :], op.add) for a in range(2)]
     _, o1 = offsets(ll, T.ll1, T.lt1, T.off1)
 
-    def dispatch(k, deps, sq, ss, lq, hand, wq_, ws_, off, between):
-        nf, nn, hc = 4 * len(far), 4 * len(near), helper(r)
+    def dispatch(k, deps, sq, ss, lq, ls, buf, hand, wq_, ws_, off):
+        def pc(to):
+            return pick_c(deps, sq, 64 * to[0], wq_, (off, 4 * to[0], 4 * len(to)))
 
         def codes(to, x):
-            return [transfer(cores[q], eng[q], "a%d%s" % (k, x), sq[:, 64 * q:64 * q + 64].bitcast(dt.uint8),
-                             lq[:, 64 * r:64 * r + 64].bitcast(dt.uint8)) for q in to]
+            tr = []
+            for q in to:
+                src = sq[:, 64 * q:64 * q + 64].bitcast(dt.uint8)
+                if q in around(r):
+                    tr.append(transfer(relay(q), eng[q], "h%d" % k, src, buf[:, 0:64].bitcast(dt.uint8)))
+                else:
+                    tr.append(transfer(cores[q], eng[q], "c%d%s" % (k, x), src, lq[:, 64 * r:64 * r + 64].bitcast(dt.uint8)))
+            return tr
 
-        def scales(q0, n, x):
-            return [transfer(hc, near_pool, "h%d%s" % (k, x), ss[:, 64 * q0:64 * q0 + 16 * n], hand[:, 64 * q0:64 * q0 + 16 * n])]
+        def go(dep, tr):
+            need("g", dep)
+            call(tr)
 
-        a, b = pick_c(deps, sq, 64 * f0, wq_, (off, 4 * f0, nf)), pick_s(deps, ss, 64 * f0, ws_, (off, 4 * f0, nf))
-        need("g", [a, b])
-        call(codes(far, "f") + scales(f0, nf, "f"))
-        between()
-        a, b = pick_c(deps, sq, 64 * n0, wq_, (off, 4 * n0, nn)), pick_s(deps, ss, 64 * n0, ws_, (off, 4 * n0, nn))
-        need("g", [b])
-        call(scales(n0, nn, "n"))
-        need("g", [a])
-        call(codes(near_to, "n"))
-        an, af = ("a%dn" % k, 2 * len(near_pool)), ("a%df" % k, 2 * len(far_pool))
-        count[an[0]], count[af[0]] = an[1], af[1]
-        return an, af
+        ahead = [[q] for q in first] if able(r) else [first]
+        sy, sn = [pick_s(deps, ss, 64 * to[0], ws_, (off, 4 * to[0], 4 * len(to))) for to in ahead + [second, near]][-2:]
+        over = [transfer(helper(r), near_pool, "h%d" % k, ss[:, 64 * f0:64 * f0 + 256], hand[:])]
+        close = [transfer(cores[q], eng_s[q], "s%dn" % k, ss[:, 64 * q:64 * q + 64], ls[:, 64 * r:64 * r + 64]) for q in near_to]
+        go([pc(ahead[0])], codes(ahead[0], "f"))
+        if able(r):
+            go([pc(ahead[1]), sy], codes(ahead[1], "f") + over)
+            go([pc(second), pc(near)], codes(second, "f") + codes(near_to, "n"))
+            go([sn], close)
+        else:
+            go([sy], over)
+            go([pc(near)], codes(near_to, "n"))
+            go([sn], close)
+            go([pc(second)], codes(second, "f"))
+        got = {}
+        for x, n in (("cn", len(near_pool)), ("sn", n_sn), ("cf", n_cf), ("sf", len(far_pool))):
+            got[x] = ("%s%d%s" % (x[0], k, x[1]), n)
+            count[got[x][0]] = n
+        return got
 
     def lists(sem, src, dst):
-        call([transfer(cores[q], eng[q][0:1], sem, src[q // 2], dst[r]) for q in far + near_to])
+        call([transfer(cores[q], one[q][0:1], sem, src[q // 2], dst[r]) for q in far + near_to])
         count[sem] = n_ranks - 1
         return (sem, n_ranks - 1)
 
     hf = 64 * (r % 2)
-    an, af = dispatch(1, o1 + [xq], T.send1, T.send1s, T.land1, T.hand1, T.xq[:], T.xs[:], T.off1, lambda: None)
+    got = dispatch(1, o1 + xq, T.send1, T.send1s, T.land1, T.land1s, T.pass1, T.hand1, T.xq[:], T.xs[:], T.off1)
     le = ts(ll, T.le[0:32, :], T.ll1[0:32, 0:16], 255.5, -4096.0, op.is_ge, op.mult)
     own = [pick_c(o1, T.land1, 64 * r, T.xq[:], (T.off1, 4 * r, 4)), pick_s(o1, T.land1s, 64 * r, T.xs[:], (T.off1, 4 * r, 4))]
     lf = tt([le], T.lf[0:32, :], T.ll1[0:32, 0:16], T.le[0:32, :], op.add)
@@ -284,100 +334,94 @@ def rank_program(g, core, T, topo):
     p2z = fill(T.p2t[:, 16:512], 0.0)
     hz = fill(T.ht[:, 2048:2056], 0.0)
     oct_ = cp([fct], T.offct[:], T.fct[:])
-    x = fill(T.rp[:, 128 * NV1:128 * NV2], 1.0)
-    thb = ts([], T.thb[:], T.i16[:], T.cf[:, 1:2], None, op.add)
+    z0 = fill(T.z2[:, :, 0:2], 0.0)
+    thb = ts([i3], T.thb[:], T.i16[:], T.cf[:, 1:2], None, op.add)
     th2 = ts([], T.th2[0:32, :], T.i16[0:32, :], T.cf[0:32, 1:2], None, op.add)
     p2r = quant([dp2, p2z], T.p2r[:], T.p2rs[:], T.p2t[:])
-    rp2 = fill(T.rp[:, 128 * NV1:128 * NV2:128], 0.0, [x])
     for b in range(4):
         p2z = quant([], T.p2q[:, 160 * b:160 * b + 128], T.p2s[:, 160 * b:160 * b + 128], zeros)
     p2q = [p2z]
     for b in range(3):
         p2q += [pick_c([p2r], T.p2q, 160 * b + 128, T.p2r[:], (T.offpl, 4 * b, 2)), pick_s([p2r], T.p2s, 160 * b + 128, T.p2rs[:], (T.offpl, 4 * b, 2))]
-    wq = quant([dw], T.wq[:], T.ws[:], T.wt[:])
 
     div = did0 = None
     mine = T.ldl1[:, hf:hf + 64, 0]
     for a in range(4):
         div = dma("y", [lst1, do1, jz], "div", T.iv[a:128:32, 0:128], mine)
-    for a in range(4):
-        did0 = dma("y", [iz], "did0", T.idw[32 * a:32 * a + 1, 0:512], mine)
+    for a in range(2):
+        did0 = dma("y", [iz], "did0", T.idw[64 * a:64 * a + 1, 0:512], mine)
+    dw = dma("y", [], "dw", T.wt[:], T.w[:])
 
     cpk = [[], [], [], []]
-    for q0, deps in ((n0, [an] + own), (f0, [af])):
+    for q0, x, y in ((n0, "n", own), (f0, "f", [None, None])):
         for t in range(4):
             c0, lo = 128 * t + 16 * q0, 64 * q0
-            cpk[t] += [pick_c(deps + [oct_], T.ctq, c0, T.land1[:, lo:lo + 256], (T.offct, 4 * t, 4)),
-                       pick_s(deps + [oct_], T.cts, c0, T.land1s[:, lo:lo + 256], (T.offct, 4 * t, 4))]
-
-    def c_t(t):
-        return T.ctq[:, 128 * t:128 * t + 128], T.cts[:, 128 * t:128 * t + 128]
-
-    sm = [mm(cpk[t] + [wvq, an, af], P[t][:], c_t(t)[0], c_t(t)[1], T.wvq[:], T.wvs[:]) for t in range(4)]
-    se = [out_of_psum(SV[t], [sm[t]], T.vt[:, t:2048:4], P[t][:], False, None) for t in range(4)]
-    vq = quant(se, T.vq[:], T.vs[:], T.vt[:])
-    aq = []
-    for h in range(2):
-        rm = [mm(own + [se[t] if h else None], P[4 - 4 * h + t][:, 0:256], c_t(t)[0], c_t(t)[1],
-                 T.land1[:, 256 * h:256 * h + 256], T.land1s[:, 256 * h:256 * h + 256]) for t in range(4)]
-        re = [out_of_psum(RV[h][t], [rm[t]], T.at[:, 1024 * h + t:1024 * h + 1024:4], P[4 - 4 * h + t][:, 0:256], True, 0.0625) for t in range(4)]
-        aq.append((quant(re, T.aq[:, 256 * h:256 * h + 256], T.asc[:, 256 * h:256 * h + 256], T.at[:, 1024 * h:1024 * h + 1024]), re))
-    om = []
-    for h in range(2):
-        om.append([mm([vq, aq[h][0]] + aq[h][1], P[4 - 4 * h + i][:, 0:256], T.vq[:, 128 * i:128 * i + 128], T.vs[:, 128 * i:128 * i + 128],
-                      T.aq[:, 256 * h:256 * h + 256], T.asc[:, 256 * h:256 * h + 256]) for i in range(4)])
-    he, hq, zt2 = [], [], [None] * 3
-    for h in range(2):
-        ev = [out_of_psum(HV[h][i], [om[h][i]], T.ht[:, 1024 * h + i:1024 * h + 1024:4], P[4 - 4 * h + i][:, 0:256], False, 0.0625) for i in range(4)]
-        he.append(ev)
-        hi = 256 if h == 0 else 514
-        hq.append(quant(ev + [hz], T.hq[:, 256 * h:hi], T.hs[:, 256 * h:hi], T.ht[:, 1024 * h:4 * hi]))
-        for b in range(3):
-            for c in (2 * h, 2 * h + 1):
-                w0 = 160 * b + 128 - 32 * c
-                zt2[b] = mm(p2q + [hq[h]] + he[0], P[4 + b][:, 0:128], T.p2q[:, w0:w0 + 128], T.p2s[:, w0:w0 + 128],
-                            T.hq[:, 128 * c:128 * c + 128], T.hs[:, 128 * c:128 * c + 128], c == 0, c == 3)
+            cpk[t] += [pick_c([got["c" + x], y[0], oct_], T.ctq, c0, T.land1[:, lo:lo + 256], (T.offct, 4 * t, 4)),
+                       pick_s([got["s" + x], y[1], oct_], T.cts, c0, T.land1s[:, lo:lo + 256], (T.offct, 4 * t, 4))]
+    landed = [got[x] for x in got] + own
+    ev, left, packed, hq = [], {}, {}, []
+    tiles = {"R": T.at, "S": T.vt, "O": T.ht}
+    for k, (kind, h, t) in enumerate(ORDER):
+        ps, lo = P[k % 8][:, 0:256], 256 * h
+        free = [ev[k - 8]] if k >= 8 else []
+        if kind == "O":
+            a, deps = (T.vq[:, 128 * t:128 * t + 128], T.vs[:, 128 * t:128 * t + 128]), [packed["S", t // 2], packed["R", h]]
+        else:
+            a, deps = (T.ctq[:, 128 * t:128 * t + 128], T.cts[:, 128 * t:128 * t + 128]), cpk[t] + landed + [wvq]
+        b = {"R": (T.land1, T.land1s), "S": (T.wvq, T.wvs), "O": (T.aq, T.asc)}[kind]
+        x = mm(deps + free, ps, a[0], a[1], b[0][:, lo:lo + 256], b[1][:, lo:lo + 256])
+        ev.append(out_of_psum(WHO[k], [x], tiles[kind][:, 4 * lo + t:4 * lo + 1024:4], ps, kind == "R", None if kind == "S" else 0.0625))
+        left.setdefault((kind, h), []).append(ev[k])
+        for y in [y for y in left if len(left[y]) == 4 and y not in packed and LATE.get(y, k) <= k]:
+            lo = 256 * y[1]
+            if y[0] == "O":
+                for a, b in (((0, 256),), ((256, 384), (384, 514)))[y[1]]:
+                    hq.append(quant(left[y] + [hz], T.hq[:, a:b], T.hs[:, a:b], T.ht[:, 4 * a:4 * b]))
+                packed[y] = hq[-1]
+            else:
+                q, sc = (T.aq, T.asc) if y[0] == "R" else (T.vq, T.vs)
+                packed[y] = quant(left[y], q[:, lo:lo + 256], sc[:, lo:lo + 256], tiles[y[0]][:, 4 * lo:4 * lo + 1024])
+    zt2 = [None] * 3
+    for c, b in [(c, b) for c in range(2) for b in range(3)] + [(2 + c, b) for c, b in LAST_TWO]:
+        w0 = 160 * b + 128 - 32 * c
+        zt2[b] = mm(p2q + [hq[max(c - 1, 0)], ev[16 + b]], P[b][:, 0:128], T.p2q[:, w0:w0 + 128], T.p2s[:, w0:w0 + 128],
+                    T.hq[:, 128 * c:128 * c + 128], T.hs[:, 128 * c:128 * c + 128], c == 0, c == 3)
     ei = s([div], T.eb[:], T.iv[:], fn.Relu, scale=-1.0, bias=1.0)
 
-    ct = running(zt2, P[4:7], T.u2, T.k2, T.eb[:], [ei])
-    last = T.k2[:, 511:512]
+    ct = running(zt2, P[0:3], T.u2, T.k2, T.eb[:], [ei])
     x2 = ts([ct, thb], T.th2[64:96, :], T.thb[64:96, :], T.k2[0:32, 511:512], T.k2[32:64, 511:512], op.subtract, op.subtract)
     x1 = ts([], T.th2[32:64, :], T.thb[32:64, :], T.k2[0:32, 511:512], None, op.subtract)
     x3 = ts([x2], T.th2[96:128, :], T.th2[64:96, :], T.k2[64:96, 511:512], None, op.subtract)
-    cv, cs = counts([x1, x3, th2, rp2], T.k2[:, 384:512], T.th2, 16, NV2, T.z2, T.zs2, T.jk2, T.acc2, T.cn2)
-    x1 = tt([cv], T.cu2[0:64, 0:NV2], T.zs2[0:64, 127:128 * NV2:128], T.zs2[64:128, 127:128 * NV2:128], op.add)
-    x2 = tt([cs], T.cu2[0:64, NV2:16], T.cn2[0:64, NV2:16], T.cn2[64:128, NV2:16], op.add)
-    ll = [tt([x1, x2], T.ll2[0:32, 16 * e:16 * e + 16], T.cu2[0:32, :], T.cu2[32:64, :], op.add) for e in range(2)]
+    cn = counts([x1, x3, th2, z0], T.k2[:, 384:512], T.th2, 16, NV2, T.z2, T.zs2, T.jk2, T.acc2, T.cn2, 1)
+    x = tt(cn, T.cu2[0:64, :], T.cn2[0:64, :], T.cn2[64:128, :], op.add)
+    ll = [tt([x], T.ll2[0:32, 16 * e:16 * e + 16], T.cu2[0:32, :], T.cu2[32:64, :], op.add) for e in range(2)]
     lt, o2 = offsets(ll, T.ll2, T.lt2, T.off2)
 
-    dl = []
-
-    def numbers():
-        o3 = [cp(lt, T.off3[32 * a:32 * a + 32, :], T.lt2[0:32, 8 * a:8 * a + 8]) for a in range(4)]
-        ids = s(o3 + [did0], T.idsel[:], T.idw[:].indirect(T.off3[:]), fn.Identity, bias=-1.0)
-        dl.append(dma("y", [ids], "dl2", T.lst2[:], T.idsel[0:128:32, :]))
-        dl.append(dma("y", [], "do2", T.ldl2[r, hf:hf + 64, 0], T.idsel[32 * (r // 2):32 * (r // 2) + 1, hf:hf + 64]))
-
-    an, af = dispatch(2, o2 + [hq[1]], T.send2, T.send2s, T.land2, T.hand2, T.hq[:], T.hs[:], T.off2, numbers)
+    got = dispatch(2, o2 + hq, T.send2, T.send2s, T.land2, T.land2s, T.pass2, T.hand2, T.hq[:], T.hs[:], T.off2)
+    o3 = [cp(lt, T.off3[64 * a:64 * a + 64, :], T.lt2[0:64, 16 * a:16 * a + 16]) for a in range(2)]
+    ids = s(o3 + [did0], T.idsel[:], T.idw[:].indirect(T.off3[:]), fn.Identity, bias=-1.0)
+    dl2 = dma("y", [ids], "dl2", T.lst2[:], T.idsel[0:128:64, :])
+    do2 = dma("y", [], "do2", T.ldl2[r, hf:hf + 64, 0], T.idsel[64 * (r // 4):64 * (r // 4) + 1, 64 * (r % 4):64 * (r % 4) + 64])
     own = [pick_c(o2, T.land2, 64 * r, T.hq[:], (T.off2, 4 * r, 4)), pick_s(o2, T.land2s, 64 * r, T.hs[:], (T.off2, 4 * r, 4))]
-    need("g", [dl[0]])
+    wq = quant([dw], T.wq[:], T.ws[:], T.wt[:])
+    need("g", [dl2])
     lst2 = lists("l2", T.lst2, T.ldl2)
 
     def ycols(b, c0, w, deps):
-        return mm([wq] + deps, b[:, 0:w], T.wq[:], T.ws[:], T.land2[:, c0:c0 + w], T.land2s[:, c0:c0 + w])
+        return mm([wq, ev[16 + b]] + deps, P[b][:, 0:w], T.wq[:], T.ws[:], T.land2[:, c0:c0 + w], T.land2s[:, c0:c0 + w])
 
-    c0, w, dn = 64 * n0, 64 * len(near), [an] + own
-    ym = ycols(P[7], c0, w, he[0] + dn)
-    dma("s", dn, "doc", T.oc[:, 4 * c0:4 * c0 + 4 * w], T.land2[:, c0:c0 + w].bitcast(dt.uint8))
-    ye = cp([ym], T.yt[:, c0:c0 + w], P[7][:, 0:w])
-    dma("s", [ye], "dy", T.y[:, c0:c0 + w], T.yt[:, c0:c0 + w])
-    c0, w = 64 * f0, 64 * len(far)
-    dma("s", [af], "doc", T.oc[:, 4 * c0:4 * c0 + 4 * w], T.land2[:, c0:c0 + w].bitcast(dt.uint8))
-    w //= 2
-    ym = [ycols(P[3 - k], c0 + w * k, w, he[1] + [af]) for k in range(2)]
-    ye = [cp([ym[0]], T.yt[:, c0:c0 + w], P[3][:, 0:w]), s([ym[1]], T.yt[:, c0 + w:c0 + 2 * w], P[2][:, 0:w], fn.Copy)]
-    dma("s", ye, "dy", T.y[:, c0:c0 + 2 * w], T.yt[:, c0:c0 + 2 * w])
+    cn, cf, w = 64 * n0, 64 * f0, 64 * len(near)
+    dma("y", [got["cn"], own[0]], "doc", T.oc[:, 4 * cn:4 * cn + 4 * w], T.land2[:, cn:cn + w].bitcast(dt.uint8))
+    dma("s", [got["cf"]], "doc", T.oc[:, 4 * cf:4 * cf + 4 * w], T.land2[:, cf:cf + w].bitcast(dt.uint8))
+    ym = ycols(3, cn, w, [got["cn"], got["sn"]] + own)
+    ye = cp([ym], T.yt[:, cn:cn + w], P[3][:, 0:w])
+    dma("y", [ye], "dy", T.y[:, cn:cn + w], T.yt[:, cn:cn + w])
     for m in range(4):
-        dma("y", dn + [af], "dos", T.osc[4 * m:4 * m + 4, :], T.land2s[32 * m:32 * m + 4, :])
-    dma("y", [lst2, dl[1]], "did", T.id[:], T.ldl2[:, hf:hf + 64, 0])
-    need("y", [(k, count[k]) for k in count])
+        dma("y", [got["sn"], got["sf"], own[1]], "dos", T.osc[4 * m:4 * m + 4, :], T.land2s[32 * m:32 * m + 4, :])
+    w //= 2
+    ym = [ycols(4 + k, cf + w * k, w, [got["cf"], got["sf"]]) for k in range(2)]
+    ye = [s([ym[0]], T.yt[:, cf:cf + w], P[4][:, 0:w], fn.Copy), cp([ym[1]], T.yt[:, cf + w:cf + 2 * w], P[5][:, 0:w])]
+    dma("s", ye, "dy", T.y[:, cf:cf + 2 * w], T.yt[:, cf:cf + 2 * w])
+    dma("y", [lst2, do2], "did", T.id[:], T.ldl2[:, hf:hf + 64, 0])
+    last = ("doc", "dos", "did", "dy")
+    need("y", [(k, count[k]) for k in count if k not in last] + [(k, count[k]) for k in last])

from concourse.bass import DstId, RemoteDMATransfer
from concourse.mybir import dt, AluOpType, ActivationFunctionType

N_CORES = 64
NR = 2
NV1, NV2 = 6, 11
ORDER = [x for t in range(4) for x in (("R", 0, t), ("S", 0, t))] + [(k, h, t) for k, h in (("S", 1), ("R", 1), ("O", 0), ("O", 1)) for t in range(4)]
WHO = "vsvsvsvssvsvsssvsvsvsssv"
LATE = {("S", 0): 11}
LAST_TWO = ((0, 0), (0, 1), (1, 0), (1, 1), (0, 2), (1, 2))

BF, H2, F4, I4, U2, CO, PL = "bfloat16", "float16", "float32", "int32", "uint16", "float8_e4m3fn_x4", "uint8"
SCRATCH = {}
for _n, _w, _d in (("zr", 128, BF), ("xt", 1032, BF), ("plt", 528, BF), ("p2t", 512, BF),
                   ("wvt", 2048, BF), ("wt", 512, BF), ("vt", 2048, BF), ("at", 2048, BF), ("ht", 2056, BF),
                   ("yt", 512, F4), ("ii", 16, I4), ("offpl", 12, U2), ("i16", 16, F4), ("i8", 8, F4), ("cf", 16, F4),
                   ("tha", 8, BF), ("th1", 8, BF), ("thb", 16, BF), ("th2", 16, BF), ("dcol", 2, BF), ("ict", 16, F4), ("fct", 16, F4),
                   ("offct", 16, U2), ("off1", 32, U2), ("off2", 32, U2), ("off3", 16, U2), ("le", 16, F4), ("lf", 16, F4), ("lid", 16, F4),
                   ("iv", 128, F4), ("eb", 128, BF), ("idw", 520, F4), ("idsel", 256, F4),
                   ("u1", 384, BF), ("k1", 512, BF), ("zs1", 2 + 64 * NV1, H2), ("jk1", 128 * (8 - NV1), BF),
                   ("acc1", 8, F4), ("cn1", 16, F4), ("ll1", 32, F4), ("lt1", 32, F4),
                   ("u2", 384, BF), ("k2", 512, BF), ("zs2", 2 + 64 * NV2, H2), ("jk2", 128 * (16 - NV2), BF),
                   ("acc2", 16, F4), ("cn2", 16, F4), ("cu2", 16, F4), ("ll2", 32, F4), ("lt2", 32, F4)):
    SCRATCH[_n] = ("sbuf", [128, _w], _d)
SCRATCH["z1"] = ("sbuf", [128, 2, 2 + 64 * NV1], BF)
SCRATCH["z2"] = ("sbuf", [128, 2, 2 + 64 * NV2], BF)
for _n, _m, _w in (("xq", "xs", 258), ("plr", "plrs", 128), ("plq", "pls", 704), ("p2r", "p2rs", 128), ("p2q", "p2s", 608), ("wvq", "wvs", 512),
                   ("wq", "ws", 128), ("send1", "send1s", 512), ("land1", "land1s", 512), ("ctq", "cts", 512), ("vq", "vs", 512),
                   ("aq", "asc", 512), ("hq", "hs", 514), ("send2", "send2s", 512), ("land2", "land2s", 512),
                   ("pass1", "hand1", 256), ("pass2", "hand2", 256)):
    SCRATCH[_n] = ("sbuf", [128, _w], CO)
    SCRATCH[_m] = ("sbuf", [128, _w], PL)
for _n, _w in (("lst1", 4), ("ldl1", 8), ("lst2", 4), ("ldl2", 8)):
    SCRATCH[_n] = ("dram", [_w, 128, 1], F4)
for _h in range(8):
    SCRATCH["ps%d" % _h] = ("psum", [128, 512], F4)
SEMAPHORES = ["v", "s", "t", "gi", "dx", "dpl", "dwv", "dw", "dp2", "dl1", "do1", "div", "did0", "dl2", "do2", "did",
              "doc", "dos", "dy", "snd", "l1", "l2", "h1", "h2", "c1n", "c1f", "s1n", "s1f", "c2n", "c2f", "s2n", "s2f"]


def rank_program(g, core, T, topo):
    cores = T.cores
    n_ranks = len(cores)

    def near_of(q):
        return [a for a in range(n_ranks) if topo.chip(cores[a]) == topo.chip(cores[q])]

    def far_of(q):
        return [a for a in range(n_ranks) if a not in near_of(q)]

    def helper(q):
        free = [c for c in topo.cores_of(cores[q]) if T.rank_of(c) is None and topo.die(c) != topo.die(cores[q])]
        return free[near_of(q).index(q)]

    def relay(q):
        can = [c for c in range(N_CORES) if topo.mates(topo.chip(c), topo.chip(cores[q])) and topo.may_write(c, cores[q])]
        i = near_of(q).index(q)
        return [c for c in can if (topo.die(c) == topo.die(cores[q])) == (i % 2 == 1)][i // 2]

    def able(q):
        return topo.may_write(cores[q], relay(far_of(q)[0]))

    def halves(q):
        far = far_of(q)
        k, w = [a for a in near_of(q) if able(a) == able(q)].index(q) % 2, len(far) // 2
        return far[w * k:w * k + w], far[w - w * k:2 * w - w * k]

    def around(q):
        return halves(q)[0][0:NR] if able(q) else []

    def pools(c, q):
        out = topo.engines(c, cores[far_of(q)[0]])
        return out, [e for e in topo.engines(c, [a for a in topo.cores_of(c) if a != c][0]) if e not in out]

    def deal(pool, to):
        w = len(pool) // len(to)
        return {q: pool[w * i:w * i + w] for i, q in enumerate(to)}

    waited, count = {}, {}

    def transfer(c, engines, sem, src, dst):
        mask = 0
        for e in engines:
            mask += 1 << e
        count["snd"] = count.get("snd", 0) + len(engines)
        rid, pid, _ = topo.addr(c)
        return RemoteDMATransfer(dst_ids=[DstId(rid=rid, pnc=pid)], dma_engine_mask=mask, remote_sem=T.sem[sem], src=src, dst=dst)

    def call(tr):
        g.remote_dma_fused(tr, local_sem=T.sem.snd)

    r = T.rank_of(core)
    if r is None:
        for q in range(n_ranks):
            if helper(q) == core:
                out, inside = pools(core, q)
                eng = deal(out, far_of(q))
                for k, (hand, land) in enumerate(((T.hand1, T.land1s), (T.hand2, T.land2s))):
                    g.wait_ge(T.sem["h%d" % (k + 1)], len(inside))
                    call([transfer(cores[e], eng[e], "s%df" % (k + 1), hand[:, 64 * i:64 * i + 64], land[:, 64 * q:64 * q + 64])
                          for i, e in enumerate(far_of(q))])
                g.wait_ge(T.sem.snd, count["snd"])
            senders = [a for a in far_of(q) if q in around(a)]
            if relay(q) == core and senders:
                out, lo = topo.engines(core, cores[q]), 64 * senders[0]
                for k, (buf, land) in enumerate(((T.pass1, T.land1), (T.pass2, T.land2))):
                    g.wait_ge(T.sem["h%d" % (k + 1)], len(out))
                    call([transfer(cores[q], out, "c%df" % (k + 1), buf[:, 0:64].bitcast(dt.uint8), land[:, lo:lo + 64].bitcast(dt.uint8))])
                g.wait_ge(T.sem.snd, count["snd"])
        return

    op, fn = AluOpType, ActivationFunctionType
    near, far = near_of(r), far_of(r)
    near_to = [near[(near.index(r) + k) % len(near)] for k in range(1, len(near))]
    n0, f0 = min(near), min(far)
    far_pool, near_pool = pools(core, r)
    wn = len(near_pool) // len(near)
    first, second = halves(r)
    eng, one = {**deal(far_pool, first), **deal(far_pool, second)}, deal(far_pool, far)
    eng_s = deal(far_pool, near_to[:-1])
    for i, q in enumerate(near_to):
        eng[q] = one[q] = near_pool[wn * i:wn * i + wn] if q in eng_s else near_pool[wn * i:]
    eng_s[near_to[-1]] = eng[near_to[-1]]
    if able(r):
        eng.update({q: far_pool for q in first})
    n_cf = sum(len(far_pool) if able(a) and r in halves(a)[0] else len(far_pool) // 2 for a in far)
    n_sn = sum(len(eng_s[q]) for q in near_to)

    Q = {"v": g.vector, "s": g.scalar, "t": g.tensor, "y": g.sync, "g": g}
    V, S, PE = g.vector, g.scalar, g.tensor

    def need(q, deps):
        best = {}
        for d in deps:
            if d is not None:
                best[d[0]] = max(best.get(d[0], 0), d[1])
        for s in best:
            if waited.get((q, s), 0) < best[s]:
                Q[q].wait_ge(T.sem[s], best[s])
                waited[(q, s)] = best[s]

    def raised(ins, s, n):
        ins.then_inc(T.sem[s], n)
        count[s] = count.get(s, 0) + n
        return (s, count[s])

    def v(deps, f, *a):
        need("v", deps)
        return raised(f(*a), "v", 1)

    def s(deps, out, in_, func, **k):
        need("s", deps)
        return raised(S.activation(out, in_, func, **k), "s", 1)

    def mm(deps, out, a, asc, b, bsc, start=True, stop=True):
        need("t", deps)
        return raised(PE.matmul_mx(out, a, asc, b, bsc, start, stop), "t", 1)

    def dma(q, deps, sem, out, in_):
        need(q, deps)
        return raised(Q[q].dma_start(out, in_), sem, 16)

    def io(pat, out, base=0, ch=0, fl=True):
        if fl:
            return raised(g.iota(out, pat, base, ch, allow_small_or_imprecise_dtypes=True), "gi", 1)
        return raised(g.iota(out, pat, base, ch), "gi", 1)

    def ts(deps, out, in0, s1, s2, *ops):
        return v(deps, V.tensor_scalar, out, in0, s1, s2, *ops)

    def tt(deps, out, a, b, o):
        return v(deps, V.tensor_tensor, out, a, b, o)

    def cp(deps, out, in_):
        return v(deps, V.tensor_copy, out, in_)

    def fill(out, c, deps=()):
        return v(list(deps), V.memset, out, c)

    def turn(deps, out, in_):
        return v(deps, V.transpose, out, in_)

    def scan(deps, *a):
        return v(deps, V.tensor_tensor_scan, *a)

    def quant(deps, q, sc, tile):
        return v(deps, V.quantize_mx, q, sc, tile)

    def pick_c(deps, dq, c0, win, off):
        n = 16 * off[2]
        return cp(deps, dq[:, c0:c0 + n].bitcast(dt.uint32), win.bitcast(dt.uint32).indirect(off[0][:, off[1]:off[1] + off[2]]))

    def pick_s(deps, ds, c0, win, off):
        n = 16 * off[2]
        return s(deps, ds[:, c0:c0 + n], win.indirect(off[0][:, off[1]:off[1] + off[2]]), fn.Copy)

    def out_of_psum(who, deps, out, ps, relu, scale):
        if who == "s":
            if scale is None:
                return s(deps, out, ps, fn.Copy)
            return s(deps, out, ps, fn.Relu if relu else fn.Identity, scale=scale)
        if scale is None:
            return cp(deps, out, ps)
        if relu:
            return ts(deps, out, ps, 0.0, scale, op.max, op.mult)
        return ts(deps, out, ps, scale, None, op.mult)

    dpl = dma("y", [], "dpl", T.plt[:, 0:16], T.pl[:, 0:16])
    dx = dma("y", [], "dx", T.xt[:, 0:1024], T.x[:])
    dwv = dma("y", [dpl], "dwv", T.wvt[:], T.wv[:])
    dp2 = dma("y", [], "dp2", T.p2t[:, 0:16], T.p2[:, 0:16])

    i0 = io([[1, 1]], T.ii[:, 0:1], 0, 1, False)
    i1 = io([[2, 8]], T.i8[:])
    zr = io([[0, 128]], T.zr[:])
    i3 = io([[1, 16]], T.i16[:])
    i2 = io([[1, 4], [64, 4]], T.ict[:])
    pz = fill(T.plt[:, 16:528], 0.0)
    xz = fill(T.xt[:, 1024:1032], 0.0)
    for b in range(3):
        opl = fill(T.offpl[:, 4 * b:4 * b + 4], b)
    zeros = T.plt[:, 16:528]
    p = T.ii[:, 0:1]
    c1 = ts([i0], T.ii[:, 1:2], p, 31, 2, op.bitwise_and, op.arith_shift_right)
    c2 = ts([], T.ii[:, 2:3], p, 3, None, op.bitwise_and)
    c3 = ts([], T.ii[:, 3:4], p, 5, 1, op.arith_shift_right, op.bitwise_and)
    for b in range(4):
        plz = quant([pz], T.plq[:, 192 * b:192 * b + 128], T.pls[:, 192 * b:192 * b + 128], zeros)
    f1 = ts([c2], T.cf[:, 1:2], T.ii[:, 2:3], 16.0, 0.5, op.mult, op.add)
    f2 = cp([c3], T.cf[:, 2:3], T.ii[:, 3:4])
    z0 = fill(T.z1[:, :, 0:2], 0.0)
    plr = quant([dpl, pz], T.plr[:], T.plrs[:], T.plt[:, 0:512])
    dcol = ts([c1], T.dcol[:, 0:1], T.ii[:, 1:2], 8.0, None, op.subtract)
    plq = [[pick_c([plr, opl], T.plq, 192 * b + 128, T.plr[:], (T.offpl, 4 * b, 4)),
            pick_s([plr, opl], T.pls, 192 * b + 128, T.plrs[:], (T.offpl, 4 * b, 4))] for b in range(3)]
    xq = [quant([dx], T.xq[:, 0:128], T.xs[:, 0:128], T.xt[:, 0:512]), quant([xz], T.xq[:, 128:258], T.xs[:, 128:258], T.xt[:, 512:1032])]
    tha = ts([i1, f1, f2], T.tha[:], T.i8[:], T.cf[:, 1:2], T.cf[:, 2:3], op.add, op.add)
    th1 = ts([], T.th1[0:64, :], T.i8[0:64, :], T.cf[0:64, 1:2], T.cf[0:64, 2:3], op.add, op.add)

    P = [T["ps%d" % b] for b in range(8)]
    zt = [None] * 3
    for h, b in LAST_TWO:
        w0 = 192 * b + 128 - 64 * h
        zt[b] = mm(plq[b] + [plz, xq[h]], P[b][:, 0:128], T.plq[:, w0:w0 + 128], T.pls[:, w0:w0 + 128],
                   T.xq[:, 128 * h:128 * h + 128], T.xs[:, 128 * h:128 * h + 128], h == 0, h == 1)

    def running(zt, zp, u, k, less, deps):
        a, b, c = [ts([zt[i]], u[:, 128 * i:128 * i + 128], zp[i][:, 0:128], 0.0, lo, op.is_lt, m)
                   for i, (lo, m) in enumerate(((-8.0, op.add), (2.0, op.mult), (4.0, op.mult)))]
        d = scan([a, b], k[:, 0:128], u[:, 128:256], u[:, 0:128], -100.0, op.max, op.add)
        e = scan([c, d], k[:, 128:256], u[:, 256:384], k[:, 0:128], -100.0, op.max, op.add)
        f = ts([e, dcol], k[:, 256:384], k[:, 128:256], T.dcol[:, 0:1], None, op.is_equal)
        return scan([f] + deps, k[:, 384:512], k[:, 256:384], less, 0.0, op.add, op.subtract)

    def counts(deps, cc, th, n, nv, z, zs, jk, acc, cn, copies):
        for a in range(nv, n):
            x = s(deps, jk[:, 128 * (a - nv):128 * (a - nv) + 128], cc, fn.Sign, bias=th[:, a:a + 1], scale=-1.0, accum_out=acc[:, a:a + 1])
        cs = [s([x], cn[:, n * e + nv:n * e + n], acc[:, nv:n], fn.Identity, scale=0.5, bias=64.0) for e in range(copies)]
        for a in range(nv):
            x = ts(deps, z[:, :, 2 + 64 * a:66 + 64 * a], cc, th[:, a:a + 1], None, op.is_le)
        x = scan([x], zs[:], z[:, 0, :], z[:, 1, :], 0.0, op.add, op.add)
        return cs + [tt([x], cn[:, n * e:n * e + nv], zs[:, 65:2 + 64 * nv:64], zs[:, 1:64 * nv - 62:64], op.subtract) for e in range(copies)]

    def offsets(deps, ll, lt, off):
        x = [turn(deps, lt[32 * a:32 * a + 32, :], ll[0:32, :]) for a in range(2)]
        return x, [cp(x, off[64 * a:64 * a + 64, :], lt[0:64, :]) for a in range(2)]

    ct = running(zt, P[0:3], T.u1, T.k1, T.zr[:], [zr])
    x = ts([ct, tha], T.th1[64:128, :], T.tha[64:128, :], T.k1[0:64, 511:512], None, op.subtract)
    cn = counts([x, th1, z0], T.k1[:, 384:512], T.th1, 8, NV1, T.z1, T.zs1, T.jk1, T.acc1, T.cn1, 2)
    ll = [tt(cn, T.ll1[0:32, a:32:2], T.cn1[32 * a:32 * a + 32, :], T.cn1[64 + 32 * a:96 + 32 * a, :], op.add) for a in range(2)]
    _, o1 = offsets(ll, T.ll1, T.lt1, T.off1)

    def dispatch(k, deps, sq, ss, lq, ls, buf, hand, wq_, ws_, off):
        def pc(to):
            return pick_c(deps, sq, 64 * to[0], wq_, (off, 4 * to[0], 4 * len(to)))

        def codes(to, x):
            tr = []
            for q in to:
                src = sq[:, 64 * q:64 * q + 64].bitcast(dt.uint8)
                if q in around(r):
                    tr.append(transfer(relay(q), eng[q], "h%d" % k, src, buf[:, 0:64].bitcast(dt.uint8)))
                else:
                    tr.append(transfer(cores[q], eng[q], "c%d%s" % (k, x), src, lq[:, 64 * r:64 * r + 64].bitcast(dt.uint8)))
            return tr

        def go(dep, tr):
            need("g", dep)
            call(tr)

        ahead = [[q] for q in first] if able(r) else [first]
        sy, sn = [pick_s(deps, ss, 64 * to[0], ws_, (off, 4 * to[0], 4 * len(to))) for to in ahead + [second, near]][-2:]
        over = [transfer(helper(r), near_pool, "h%d" % k, ss[:, 64 * f0:64 * f0 + 256], hand[:])]
        close = [transfer(cores[q], eng_s[q], "s%dn" % k, ss[:, 64 * q:64 * q + 64], ls[:, 64 * r:64 * r + 64]) for q in near_to]
        go([pc(ahead[0])], codes(ahead[0], "f"))
        if able(r):
            go([pc(ahead[1]), sy], codes(ahead[1], "f") + over)
            go([pc(second), pc(near)], codes(second, "f") + codes(near_to, "n"))
            go([sn], close)
        else:
            go([sy], over)
            go([pc(near)], codes(near_to, "n"))
            go([sn], close)
            go([pc(second)], codes(second, "f"))
        got = {}
        for x, n in (("cn", len(near_pool)), ("sn", n_sn), ("cf", n_cf), ("sf", len(far_pool))):
            got[x] = ("%s%d%s" % (x[0], k, x[1]), n)
            count[got[x][0]] = n
        return got

    def lists(sem, src, dst):
        call([transfer(cores[q], one[q][0:1], sem, src[q // 2], dst[r]) for q in far + near_to])
        count[sem] = n_ranks - 1
        return (sem, n_ranks - 1)

    hf = 64 * (r % 2)
    got = dispatch(1, o1 + xq, T.send1, T.send1s, T.land1, T.land1s, T.pass1, T.hand1, T.xq[:], T.xs[:], T.off1)
    le = ts(ll, T.le[0:32, :], T.ll1[0:32, 0:16], 255.5, -4096.0, op.is_ge, op.mult)
    own = [pick_c(o1, T.land1, 64 * r, T.xq[:], (T.off1, 4 * r, 4)), pick_s(o1, T.land1s, 64 * r, T.xs[:], (T.off1, 4 * r, 4))]
    lf = tt([le], T.lf[0:32, :], T.ll1[0:32, 0:16], T.le[0:32, :], op.add)
    lid = s([lf], T.lid[0:32, :], T.lf[0:32, :], fn.Relu, bias=float(256 * r + 1))
    dl1 = dma("y", [lid], "dl1", T.lst1[:], T.lid[0:32, 0:16])
    do1 = dma("y", [], "do1", T.ldl1[r, hf:hf + 64, 0], T.lid[4 * r:4 * r + 4, 0:16])
    need("g", [dl1])
    lst1 = lists("l1", T.lst1, T.ldl1)

    c4 = ts([], T.ii[:, 4:5], p, 15, None, op.bitwise_and)
    iz = fill(T.idw[:], 0.0)
    jz = fill(T.iv[:], 1.0)
    f4 = ts([c4], T.cf[:, 4:5], T.ii[:, 4:5], 4.0, None, op.mult)
    wvq = quant([dwv], T.wvq[:], T.wvs[:], T.wvt[:])
    fct = s([i2, f4], T.fct[:], T.ict[:], fn.Identity, bias=T.cf[:, 4:5])
    p2z = fill(T.p2t[:, 16:512], 0.0)
    hz = fill(T.ht[:, 2048:2056], 0.0)
    oct_ = cp([fct], T.offct[:], T.fct[:])
    z0 = fill(T.z2[:, :, 0:2], 0.0)
    thb = ts([i3], T.thb[:], T.i16[:], T.cf[:, 1:2], None, op.add)
    th2 = ts([], T.th2[0:32, :], T.i16[0:32, :], T.cf[0:32, 1:2], None, op.add)
    p2r = quant([dp2, p2z], T.p2r[:], T.p2rs[:], T.p2t[:])
    for b in range(4):
        p2z = quant([], T.p2q[:, 160 * b:160 * b + 128], T.p2s[:, 160 * b:160 * b + 128], zeros)
    p2q = [p2z]
    for b in range(3):
        p2q += [pick_c([p2r], T.p2q, 160 * b + 128, T.p2r[:], (T.offpl, 4 * b, 2)), pick_s([p2r], T.p2s, 160 * b + 128, T.p2rs[:], (T.offpl, 4 * b, 2))]

    div = did0 = None
    mine = T.ldl1[:, hf:hf + 64, 0]
    for a in range(4):
        div = dma("y", [lst1, do1, jz], "div", T.iv[a:128:32, 0:128], mine)
    for a in range(2):
        did0 = dma("y", [iz], "did0", T.idw[64 * a:64 * a + 1, 0:512], mine)
    dw = dma("y", [], "dw", T.wt[:], T.w[:])

    cpk = [[], [], [], []]
    for q0, x, y in ((n0, "n", own), (f0, "f", [None, None])):
        for t in range(4):
            c0, lo = 128 * t + 16 * q0, 64 * q0
            cpk[t] += [pick_c([got["c" + x], y[0], oct_], T.ctq, c0, T.land1[:, lo:lo + 256], (T.offct, 4 * t, 4)),
                       pick_s([got["s" + x], y[1], oct_], T.cts, c0, T.land1s[:, lo:lo + 256], (T.offct, 4 * t, 4))]
    landed = [got[x] for x in got] + own
    ev, left, packed, hq = [], {}, {}, []
    tiles = {"R": T.at, "S": T.vt, "O": T.ht}
    for k, (kind, h, t) in enumerate(ORDER):
        ps, lo = P[k % 8][:, 0:256], 256 * h
        free = [ev[k - 8]] if k >= 8 else []
        if kind == "O":
            a, deps = (T.vq[:, 128 * t:128 * t + 128], T.vs[:, 128 * t:128 * t + 128]), [packed["S", t // 2], packed["R", h]]
        else:
            a, deps = (T.ctq[:, 128 * t:128 * t + 128], T.cts[:, 128 * t:128 * t + 128]), cpk[t] + landed + [wvq]
        b = {"R": (T.land1, T.land1s), "S": (T.wvq, T.wvs), "O": (T.aq, T.asc)}[kind]
        x = mm(deps + free, ps, a[0], a[1], b[0][:, lo:lo + 256], b[1][:, lo:lo + 256])
        ev.append(out_of_psum(WHO[k], [x], tiles[kind][:, 4 * lo + t:4 * lo + 1024:4], ps, kind == "R", None if kind == "S" else 0.0625))
        left.setdefault((kind, h), []).append(ev[k])
        for y in [y for y in left if len(left[y]) == 4 and y not in packed and LATE.get(y, k) <= k]:
            lo = 256 * y[1]
            if y[0] == "O":
                for a, b in (((0, 256),), ((256, 384), (384, 514)))[y[1]]:
                    hq.append(quant(left[y] + [hz], T.hq[:, a:b], T.hs[:, a:b], T.ht[:, 4 * a:4 * b]))
                packed[y] = hq[-1]
            else:
                q, sc = (T.aq, T.asc) if y[0] == "R" else (T.vq, T.vs)
                packed[y] = quant(left[y], q[:, lo:lo + 256], sc[:, lo:lo + 256], tiles[y[0]][:, 4 * lo:4 * lo + 1024])
    zt2 = [None] * 3
    for c, b in [(c, b) for c in range(2) for b in range(3)] + [(2 + c, b) for c, b in LAST_TWO]:
        w0 = 160 * b + 128 - 32 * c
        zt2[b] = mm(p2q + [hq[max(c - 1, 0)], ev[16 + b]], P[b][:, 0:128], T.p2q[:, w0:w0 + 128], T.p2s[:, w0:w0 + 128],
                    T.hq[:, 128 * c:128 * c + 128], T.hs[:, 128 * c:128 * c + 128], c == 0, c == 3)
    ei = s([div], T.eb[:], T.iv[:], fn.Relu, scale=-1.0, bias=1.0)

    ct = running(zt2, P[0:3], T.u2, T.k2, T.eb[:], [ei])
    x2 = ts([ct, thb], T.th2[64:96, :], T.thb[64:96, :], T.k2[0:32, 511:512], T.k2[32:64, 511:512], op.subtract, op.subtract)
    x1 = ts([], T.th2[32:64, :], T.thb[32:64, :], T.k2[0:32, 511:512], None, op.subtract)
    x3 = ts([x2], T.th2[96:128, :], T.th2[64:96, :], T.k2[64:96, 511:512], None, op.subtract)
    cn = counts([x1, x3, th2, z0], T.k2[:, 384:512], T.th2, 16, NV2, T.z2, T.zs2, T.jk2, T.acc2, T.cn2, 1)
    x = tt(cn, T.cu2[0:64, :], T.cn2[0:64, :], T.cn2[64:128, :], op.add)
    ll = [tt([x], T.ll2[0:32, 16 * e:16 * e + 16], T.cu2[0:32, :], T.cu2[32:64, :], op.add) for e in range(2)]
    lt, o2 = offsets(ll, T.ll2, T.lt2, T.off2)

    got = dispatch(2, o2 + hq, T.send2, T.send2s, T.land2, T.land2s, T.pass2, T.hand2, T.hq[:], T.hs[:], T.off2)
    o3 = [cp(lt, T.off3[64 * a:64 * a + 64, :], T.lt2[0:64, 16 * a:16 * a + 16]) for a in range(2)]
    ids = s(o3 + [did0], T.idsel[:], T.idw[:].indirect(T.off3[:]), fn.Identity, bias=-1.0)
    dl2 = dma("y", [ids], "dl2", T.lst2[:], T.idsel[0:128:64, :])
    do2 = dma("y", [], "do2", T.ldl2[r, hf:hf + 64, 0], T.idsel[64 * (r // 4):64 * (r // 4) + 1, 64 * (r % 4):64 * (r % 4) + 64])
    own = [pick_c(o2, T.land2, 64 * r, T.hq[:], (T.off2, 4 * r, 4)), pick_s(o2, T.land2s, 64 * r, T.hs[:], (T.off2, 4 * r, 4))]
    wq = quant([dw], T.wq[:], T.ws[:], T.wt[:])
    need("g", [dl2])
    lst2 = lists("l2", T.lst2, T.ldl2)

    def ycols(b, c0, w, deps):
        return mm([wq, ev[16 + b]] + deps, P[b][:, 0:w], T.wq[:], T.ws[:], T.land2[:, c0:c0 + w], T.land2s[:, c0:c0 + w])

    cn, cf, w = 64 * n0, 64 * f0, 64 * len(near)
    dma("y", [got["cn"], own[0]], "doc", T.oc[:, 4 * cn:4 * cn + 4 * w], T.land2[:, cn:cn + w].bitcast(dt.uint8))
    dma("s", [got["cf"]], "doc", T.oc[:, 4 * cf:4 * cf + 4 * w], T.land2[:, cf:cf + w].bitcast(dt.uint8))
    ym = ycols(3, cn, w, [got["cn"], got["sn"]] + own)
    ye = cp([ym], T.yt[:, cn:cn + w], P[3][:, 0:w])
    dma("y", [ye], "dy", T.y[:, cn:cn + w], T.yt[:, cn:cn + w])
    for m in range(4):
        dma("y", [got["sn"], got["sf"], own[1]], "dos", T.osc[4 * m:4 * m + 4, :], T.land2s[32 * m:32 * m + 4, :])
    w //= 2
    ym = [ycols(4 + k, cf + w * k, w, [got["cf"], got["sf"]]) for k in range(2)]
    ye = [s([ym[0]], T.yt[:, cf:cf + w], P[4][:, 0:w], fn.Copy), cp([ym[1]], T.yt[:, cf + w:cf + 2 * w], P[5][:, 0:w])]
    dma("s", ye, "dy", T.y[:, cf:cf + 2 * w], T.yt[:, cf:cf + 2 * w])
    dma("y", [lst2, do2], "did", T.id[:], T.ldl2[:, hf:hf + 64, 0])
    last = ("doc", "dos", "did", "dy")
    need("y", [(k, count[k]) for k in count if k not in last] + [(k, count[k]) for k in last])
